import numpy as np
import ml_dtypes


def mxq(x, axis, fmt="e4m3"):
    dtype, down = {"e4m3": (ml_dtypes.float8_e4m3fn, 7), "e5m2": (ml_dtypes.float8_e5m2, 14)}[fmt]
    v = np.moveaxis(np.asarray(x, np.float32).astype(ml_dtypes.bfloat16).astype(np.float64), axis, -1)
    blocks = v.reshape(v.shape[:-1] + (-1, 32))
    amax = np.abs(blocks).max(-1, keepdims=True)
    byte = np.maximum(np.where(amax > 0, np.frexp(amax)[1] - 1 + 127, 0) - down, 1)
    scale = np.exp2(byte - 127.0)
    codes = (blocks / scale).astype(np.float32).astype(dtype).astype(np.float64)
    return np.moveaxis((codes * scale).reshape(v.shape), -1, axis)


WIDE = False


def mx_kscale(k):
    if not WIDE:
        return np.ones(k)
    levels = np.array([10, -10, 5, -5, 0])
    if k % 512:
        return np.exp2(np.random.permutation(np.resize(levels, k // 32))).repeat(32)
    a = np.empty((k // 512, 16))
    for p in range(k // 512):
        a[p, :8] = np.random.permutation(np.resize(levels, 8))
        for g in range(8):
            far = levels[np.abs(levels - a[p, g]) >= 10]
            a[p, g + 8] = far[np.random.randint(len(far))]
    return np.exp2(a.ravel()).repeat(32)


def f64(x):
    return np.asarray(x).astype(np.float64)


def striped(idx):
    return np.tile(idx.reshape(-1, 16).T, (8, 1)).astype(np.uint16)


def unstriped(offs):
    return offs[:16].T.reshape(-1).astype(np.int64)


E2M1 = np.array([0.0, 0.5, 1.0, 1.5, 2.0, 3.0, 4.0, 6.0, -0.0, -0.5, -1.0, -1.5, -2.0, -3.0, -4.0, -6.0])


def pack_weight(w, fmt):
    k, n = w.shape
    w = f64(np.asarray(w, np.float32).astype(ml_dtypes.bfloat16)).reshape(k // 32, 32, n)
    amax = np.abs(w).max(1)
    if fmt == "e4m3":
        byte = np.frexp(amax)[1] - 1 + 127 - 7
    else:
        mant, ex = np.frexp(amax / 6.0)
        byte = np.where(mant > 0.5, ex, ex - 1) + 127
    byte = np.clip(np.where(amax > 0, byte, 1), 1, 254)
    scaled = (w * np.exp2(127.0 - byte)[:, None, :]).reshape(k, n).astype(np.float32)
    by_word = np.ascontiguousarray(scaled.reshape(k // 512, 128, 4, n).transpose(0, 1, 3, 2))
    if fmt == "e4m3":
        words = by_word.astype(ml_dtypes.float8_e4m3fn).view(np.uint8)
    else:
        c = by_word.astype(ml_dtypes.float4_e2m1fn).view(np.uint8) & 0xF
        words = (c[..., 0::2] | (c[..., 1::2] << 4)).reshape(k // 512, 128, 2 * n)
    return np.ascontiguousarray(words), np.ascontiguousarray(byte.astype(np.uint8).reshape(k // 512, 16, n))


def unpack_weight(words, scales, fmt):
    g, _, n = scales.shape
    words = np.ascontiguousarray(words).reshape(g, 128, n, -1)
    if fmt == "e4m3":
        vals = words.view(ml_dtypes.float8_e4m3fn).astype(np.float64)
    else:
        nib = np.empty((g, 128, n, 4), np.uint8)
        nib[..., 0::2] = words & 0xF
        nib[..., 1::2] = words >> 4
        vals = E2M1[nib]
    vals = vals * np.repeat(np.exp2(scales.astype(np.float64) - 127.0), 8, axis=1)[..., None]
    return vals.transpose(0, 1, 3, 2).reshape(g * 512, n)


def gelu(v):
    return 0.5 * v * (1.0 + np.tanh(np.sqrt(2.0 / np.pi) * (v + 0.044715 * v**3)))


K, T, S, T2, H, N = 1024, 4096, 1024, 2048, 512, 512

def setup_inputs():
    n = np.random.standard_normal
    s = mx_kscale(K)[:, None]
    u = mx_kscale(H)[:, None]
    tab_words, tab_scales = pack_weight(n((K, T)) * s, "e4m3")
    w4_words, w4_scales = pack_weight(n((H, N)) / np.sqrt(H) / u, "e2m1")
    return {
        "tab_words": tab_words,
        "tab_scales": tab_scales,
        "offs": striped(np.random.permutation(T)[:S]),
        "offs2": striped(np.random.permutation(T2)[:S]),
        "w1": (1.5 * n((K, H)) / np.sqrt(K) / s).astype(np.float32),
        "wgs": np.exp(0.3 * n((128, S))).astype(np.float32),
        "base": (n((H, T2)) * u).astype(np.float32),
        "w4_words": w4_words,
        "w4_scales": w4_scales,
    }

def reference(tab_words, tab_scales, offs, offs2, w1, wgs, base, w4_words, w4_scales):
    v = unpack_weight(tab_words, tab_scales, "e4m3")[:, unstriped(offs)]
    y = mxq(f64(w1), 0, "e4m3").T @ v
    h = np.log(1.0 + np.abs(y))
    page = np.zeros((H, T2))
    page[:, unstriped(offs2)] = np.tile(f64(wgs), (H // 128, 1)) * h
    z = f64(base) * np.exp(-page)
    zq = mxq(z, 0, "e4m3")
    w4 = unpack_weight(w4_words, w4_scales, "e2m1")
    return w4.T @ zq

@@ -1,0 +1,206 @@
+from contextlib import ExitStack
+
+import concourse.mybir as mybir
+
+K, T, S, T2, H, N = 1024, 4096, 1024, 2048, 512, 512
+FLOPS = 2 * K * H * S + 2 * H * N * T2
+
+F32 = mybir.dt.float32
+BF16 = mybir.dt.bfloat16
+I32 = mybir.dt.int32
+U32 = mybir.dt.uint32
+U16 = mybir.dt.uint16
+U8 = mybir.dt.uint8
+FP8X4 = mybir.dt.float8_e4m3fn_x4
+FP4X4 = mybir.dt.float4_e2m1fn_x4
+ACT = mybir.ActivationFunctionType
+MULT = mybir.AluOpType.mult
+
+P = 128
+PACK = 4
+QUAD = 32
+PASSES = K // (P * PACK)
+BANK = 512
+HALVES = S // BANK
+PER_COL = 16
+PAGES = 3
+CHUNKS = (256, 512, 512, 512, 256)
+FIRST_PIECES = (256, 256, 512)
+
+
+def tile_list_speech_noise_suppression_kernel(
+    tc, tab_words, tab_scales, offs, offs2, w1, wgs, base, w4_words, w4_scales, out
+):
+    nc = tc.nc
+    with ExitStack() as ctx:
+        keep = ctx.enter_context(tc.tile_pool(name="keep", bufs=1))
+        ring = ctx.enter_context(tc.tile_pool(name="ring", bufs=2))
+        stage = ctx.enter_context(tc.tile_pool(name="stage", bufs=6))
+        psum = ctx.enter_context(tc.psum_pool(name="psum", bufs=8))
+
+        tab_s = keep.tile([P, T], U8, name="tab_s", align_bytes=64)
+        nc.sync.dma_start(
+            out=tab_s[0:QUAD, :].bitcast(I32), in_=tab_scales.rearrange("a q t -> q a t").bitcast(I32)
+        )
+        nc.vector.memset(tab_s[QUAD : 2 * QUAD, :].bitcast(I32), 0)
+        nc.vector.memset(tab_s[2 * QUAD : P, :].bitcast(I32), 0)
+        v_s = keep.tile([P, PASSES * S], U8, name="v_s", align_bytes=64)
+        nc.vector.memset(v_s[:].bitcast(I32), 0)
+        w4_s = keep.tile([P, N], U8, name="w4_s", align_bytes=64)
+        nc.vector.memset(w4_s[:].bitcast(I32), 0)
+        warm = keep.tile([P, 2], F32, name="warm")
+        nc.vector.memset(warm[:, 0:1], 1.0)
+        nc.scalar.activation(out=warm[:, 1:2], in_=warm[:, 0:1], func=ACT.Ln)
+        pages = [keep.tile([P, T2], F32, name=f"page{u}") for u in range(PAGES)]
+        for page in pages:
+            nc.vector.memset(page[:], 0.0)
+
+        pick = keep.tile([P, S // PER_COL], U16, name="pick")
+        nc.sync.dma_start(pick[:], offs)
+        tab_w = [keep.tile([P, T], I32, name=f"tab_w{a}", align_bytes=64) for a in range(PASSES)]
+        nc.sync.dma_start(out=tab_w[0][:], in_=tab_words[0].rearrange("p n i -> p (n i)").bitcast(I32))
+        w1_raw = [keep.tile([P, PACK, H], F32, name=f"w1_raw{a}") for a in range(PASSES)]
+        for a in range(PASSES):
+            nc.sync.dma_start(
+                out=w1_raw[a][:],
+                in_=w1[a * P * PACK : (a + 1) * P * PACK, :].rearrange("(p j) c -> p j c", j=PACK),
+            )
+        nc.sync.dma_start(out=tab_w[1][:], in_=tab_words[1].rearrange("p n i -> p (n i)").bitcast(I32))
+        place = keep.tile([P, S // PER_COL], U16, name="place")
+        nc.sync.dma_start(place[:], offs2)
+        wgs_rows = wgs.rearrange("(p t) j -> p t j", t=PACK)
+        wg_first = keep.tile([P, S], F32, name="wg_first")
+        wg_rest = keep.tile([P, PACK - 1, S], F32, name="wg_rest")
+        for q in (0, 2, 1, 3):
+            nc.sync.dma_start(out=wg_first[QUAD * q : QUAD * (q + 1), :], in_=wgs_rows[:, 0, :])
+        for q in (0, 2, 1, 3):
+            nc.sync.dma_start(out=wg_rest[QUAD * q : QUAD * (q + 1), :, :], in_=wgs_rows[:, 1:PACK, :])
+        w4_w = keep.tile([P, 2 * N], U8, name="w4_w", align_bytes=64)
+        nc.sync.dma_start(out=w4_w[:].bitcast(I32), in_=w4_words[0].bitcast(I32))
+        for q in range(P // QUAD):
+            nc.sync.dma_start(
+                out=w4_s[QUAD * q : QUAD * q + 4, :].bitcast(I32),
+                in_=w4_scales[0, 4 * q : 4 * q + 4, :].bitcast(I32),
+            )
+        base_rows = base.rearrange("(p t) c -> p t c", t=PACK)
+        starts = [sum(CHUNKS[:i]) for i in range(len(CHUNKS))]
+        base_sb = [keep.tile([P, PACK, w], F32, name=f"base{i}") for i, w in enumerate(CHUNKS)]
+        for i, w in enumerate(CHUNKS):
+            nc.sync.dma_start(out=base_sb[i][:], in_=base_rows[:, :, starts[i] : starts[i] + w])
+
+        picked_s = keep.tile([P, S], U8, name="picked_s", align_bytes=64)
+        nc.vector.tensor_copy(out=picked_s[:], in_=tab_s[:].indirect(pick[:]))
+        for q in range(P // QUAD):
+            nc.gpsimd.dma_start(
+                out=v_s[QUAD * q : QUAD * q + 4, :].bitcast(I32),
+                in_=picked_s[8 * q : 8 * q + 8, :].bitcast(I32),
+            )
+
+        v_first = keep.tile([P, S], U32, name="v_first", align_bytes=64)
+        nc.vector.tensor_copy(out=v_first[:], in_=tab_w[0][:].bitcast(U32).indirect(pick[:]))
+
+        w1_c = [keep.tile([P, H], U32, name=f"w1_c{a}", align_bytes=64) for a in range(PASSES)]
+        w1_s = [keep.tile([P, H], U8, name=f"w1_s{a}", align_bytes=64) for a in range(PASSES)]
+        for a in range(PASSES):
+            grouped = ring.tile([P, PACK * H], BF16, name="grouped", align_bytes=64)
+            nc.vector.tensor_copy(
+                out=grouped[:].rearrange("p (t m j) -> p m j t", t=PACK, j=PACK),
+                in_=w1_raw[a][:].rearrange("p j (m t) -> p m j t", t=PACK),
+            )
+            nc.vector.quantize_mx(out=w1_c[a][:].bitcast(FP8X4), scales=w1_s[a][:], in_=grouped[:])
+
+        v_last = [keep.tile([P, BANK], U32, name=f"v_last{b}", align_bytes=64) for b in range(HALVES)]
+        cols_per_half = BANK // PER_COL
+        for b in range(HALVES):
+            nc.vector.tensor_copy(
+                out=v_last[b][:],
+                in_=tab_w[1][:].bitcast(U32).indirect(pick[:, b * cols_per_half : (b + 1) * cols_per_half]),
+            )
+
+        y = {}
+        for t in range(PACK):
+            for b in range(HALVES):
+                y[t, b] = psum.tile([P, BANK], F32, name="bank")
+                nc.tensor.matmul_mx(
+                    out=y[t, b][:],
+                    lhsT=w1_c[0][:, t * P : (t + 1) * P].bitcast(FP8X4),
+                    lhsT_scale=w1_s[0][:, t * P : (t + 1) * P],
+                    rhs=v_first[:, b * BANK : (b + 1) * BANK].bitcast(FP8X4),
+                    rhs_scale=v_s[:, b * BANK : (b + 1) * BANK],
+                    start=True,
+                    stop=False,
+                )
+        for t in range(PACK):
+            for b in range(HALVES):
+                nc.tensor.matmul_mx(
+                    out=y[t, b][:],
+                    lhsT=w1_c[1][:, t * P : (t + 1) * P].bitcast(FP8X4),
+                    lhsT_scale=w1_s[1][:, t * P : (t + 1) * P],
+                    rhs=v_last[b][:].bitcast(FP8X4),
+                    rhs_scale=v_s[:, S + b * BANK : S + (b + 1) * BANK],
+                    start=False,
+                    stop=True,
+                )
+
+        h = [keep.tile([P, S], F32, name=f"h{t}") for t in range(PACK)]
+        pieces = [FIRST_PIECES] + [(BANK,) * HALVES] * (PACK - 1)
+        for t in range(PACK):
+            j0 = 0
+            for w in pieces[t]:
+                b, c0 = divmod(j0, BANK)
+                nc.scalar.activation(out=h[t][:, j0 : j0 + w], in_=y[t, b][:, c0 : c0 + w], func=ACT.Abs)
+                nc.scalar.activation(out=h[t][:, j0 : j0 + w], in_=h[t][:, j0 : j0 + w], func=ACT.Ln, bias=1.0)
+                j0 += w
+
+        gain = [keep.tile([P, PACK, w], F32, name=f"gain{i}") for i, w in enumerate(CHUNKS)]
+        for t in range(PACK):
+            page = pages[t % PAGES]
+            weights = wg_first[:] if t == 0 else wg_rest[:, t - 1, :]
+            j0 = 0
+            for w in FIRST_PIECES if t == 0 else (S,):
+                nc.vector.tensor_tensor(
+                    out=page[:].indirect(place[:, j0 // PER_COL : (j0 + w) // PER_COL]),
+                    in0=h[t][:, j0 : j0 + w],
+                    in1=weights[:, j0 : j0 + w],
+                    op=MULT,
+                )
+                j0 += w
+            for i, w in enumerate(CHUNKS):
+                nc.scalar.activation(
+                    out=gain[i][:, t, :], in_=page[:, starts[i] : starts[i] + w], func=ACT.Exp, scale=-1.0
+                )
+
+        out_rows = out.rearrange("(g p) c -> p g c", p=P)
+        for i, w in enumerate(CHUNKS):
+            z = ring.tile([P, PACK * w], BF16, name="z", align_bytes=64)
+            nc.vector.tensor_tensor(
+                out=z[:].rearrange("p (c e t) -> p c t e", e=4, t=PACK),
+                in0=gain[i][:].rearrange("p t (c e) -> p c t e", e=4),
+                in1=base_sb[i][:].rearrange("p t (c e) -> p c t e", e=4),
+                op=MULT,
+            )
+            z_c = ring.tile([P, w], U32, name="z_c", align_bytes=64)
+            z_s = ring.tile([P, w], U8, name="z_s", align_bytes=64)
+            nc.vector.quantize_mx(out=z_c[:].bitcast(FP8X4), scales=z_s[:], in_=z[:])
+            per_bank = BANK // w
+            for g0 in range(0, N // P, per_bank):
+                acc = psum.tile([P, BANK], F32, name="bank")
+                for g in range(g0, g0 + per_bank):
+                    nc.tensor.matmul_mx(
+                        out=acc[:, (g - g0) * w : (g - g0 + 1) * w],
+                        lhsT=w4_w[:, 2 * g * P : 2 * (g + 1) * P].bitcast(FP4X4),
+                        lhsT_scale=w4_s[:, g * P : (g + 1) * P],
+                        rhs=z_c[:].bitcast(FP8X4),
+                        rhs_scale=z_s[:],
+                        start=True,
+                        stop=True,
+                    )
+                res = stage.tile([P, BANK], F32, name="res")
+                if i == len(CHUNKS) - 1 and g0 == 0:
+                    nc.vector.tensor_copy(out=res[:], in_=acc[:])
+                else:
+                    nc.scalar.copy(out=res[:], in_=acc[:])
+                nc.sync.dma_start(
+                    out=out_rows[:, g0 : g0 + per_bank, starts[i] : starts[i] + w],
+                    in_=res[:].rearrange("p (g c) -> p g c", g=per_bank),
+                )

@@ -24,7 +24,8 @@ BANK = 512
 HALVES = S // BANK
 PER_COL = 16
 PAGES = 3
-CHUNKS = (256, 512, 512, 512, 256)
+CHUNKS = (256,) * 8
+BASE_LOADS = (256, 512, 512, 512, 256)
 FIRST_PIECES = (256, 256, 512)
 
 
@@ -35,31 +36,18 @@ def tile_list_speech_noise_suppression_kernel(
     with ExitStack() as ctx:
         keep = ctx.enter_context(tc.tile_pool(name="keep", bufs=1))
         ring = ctx.enter_context(tc.tile_pool(name="ring", bufs=2))
-        stage = ctx.enter_context(tc.tile_pool(name="stage", bufs=6))
+        stage = ctx.enter_context(tc.tile_pool(name="stage", bufs=16))
         psum = ctx.enter_context(tc.psum_pool(name="psum", bufs=8))
 
         tab_s = keep.tile([P, T], U8, name="tab_s", align_bytes=64)
         nc.sync.dma_start(
             out=tab_s[0:QUAD, :].bitcast(I32), in_=tab_scales.rearrange("a q t -> q a t").bitcast(I32)
         )
-        nc.vector.memset(tab_s[QUAD : 2 * QUAD, :].bitcast(I32), 0)
-        nc.vector.memset(tab_s[2 * QUAD : P, :].bitcast(I32), 0)
-        v_s = keep.tile([P, PASSES * S], U8, name="v_s", align_bytes=64)
-        nc.vector.memset(v_s[:].bitcast(I32), 0)
-        w4_s = keep.tile([P, N], U8, name="w4_s", align_bytes=64)
-        nc.vector.memset(w4_s[:].bitcast(I32), 0)
-        warm = keep.tile([P, 2], F32, name="warm")
-        nc.vector.memset(warm[:, 0:1], 1.0)
-        nc.scalar.activation(out=warm[:, 1:2], in_=warm[:, 0:1], func=ACT.Ln)
-        pages = [keep.tile([P, T2], F32, name=f"page{u}") for u in range(PAGES)]
-        for page in pages:
-            nc.vector.memset(page[:], 0.0)
-
         pick = keep.tile([P, S // PER_COL], U16, name="pick")
         nc.sync.dma_start(pick[:], offs)
-        tab_w = [keep.tile([P, T], I32, name=f"tab_w{a}", align_bytes=64) for a in range(PASSES)]
+        tab_w = [keep.tile([P, T], I32, name=f"tab_w{a}", tag=f"table{a}", align_bytes=64) for a in range(PASSES)]
         nc.sync.dma_start(out=tab_w[0][:], in_=tab_words[0].rearrange("p n i -> p (n i)").bitcast(I32))
-        w1_raw = [keep.tile([P, PACK, H], F32, name=f"w1_raw{a}") for a in range(PASSES)]
+        w1_raw = [keep.tile([P, PACK, H], F32, name=f"w1_raw{a}", tag=f"raw{a}") for a in range(PASSES)]
         for a in range(PASSES):
             nc.sync.dma_start(
                 out=w1_raw[a][:],
@@ -68,41 +56,34 @@ def tile_list_speech_noise_suppression_kernel(
         nc.sync.dma_start(out=tab_w[1][:], in_=tab_words[1].rearrange("p n i -> p (n i)").bitcast(I32))
         place = keep.tile([P, S // PER_COL], U16, name="place")
         nc.sync.dma_start(place[:], offs2)
-        wgs_rows = wgs.rearrange("(p t) j -> p t j", t=PACK)
-        wg_first = keep.tile([P, S], F32, name="wg_first")
-        wg_rest = keep.tile([P, PACK - 1, S], F32, name="wg_rest")
-        for q in (0, 2, 1, 3):
-            nc.sync.dma_start(out=wg_first[QUAD * q : QUAD * (q + 1), :], in_=wgs_rows[:, 0, :])
-        for q in (0, 2, 1, 3):
-            nc.sync.dma_start(out=wg_rest[QUAD * q : QUAD * (q + 1), :, :], in_=wgs_rows[:, 1:PACK, :])
-        w4_w = keep.tile([P, 2 * N], U8, name="w4_w", align_bytes=64)
-        nc.sync.dma_start(out=w4_w[:].bitcast(I32), in_=w4_words[0].bitcast(I32))
-        for q in range(P // QUAD):
-            nc.sync.dma_start(
-                out=w4_s[QUAD * q : QUAD * q + 4, :].bitcast(I32),
-                in_=w4_scales[0, 4 * q : 4 * q + 4, :].bitcast(I32),
-            )
-        base_rows = base.rearrange("(p t) c -> p t c", t=PACK)
-        starts = [sum(CHUNKS[:i]) for i in range(len(CHUNKS))]
-        base_sb = [keep.tile([P, PACK, w], F32, name=f"base{i}") for i, w in enumerate(CHUNKS)]
-        for i, w in enumerate(CHUNKS):
-            nc.sync.dma_start(out=base_sb[i][:], in_=base_rows[:, :, starts[i] : starts[i] + w])
 
-        picked_s = keep.tile([P, S], U8, name="picked_s", align_bytes=64)
+        nc.gpsimd.memset(tab_s[QUAD : 2 * QUAD, :].bitcast(I32), 0)
+        nc.gpsimd.memset(tab_s[2 * QUAD : P, :].bitcast(I32), 0)
+        v_s = keep.tile([P, PASSES * S], U8, name="v_s", align_bytes=64)
+        nc.vector.memset(v_s[:].bitcast(I32), 0)
+        warm = keep.tile([P, 2], F32, name="warm")
+        nc.vector.memset(warm[:, 0:1], 1.0)
+        nc.scalar.activation(out=warm[:, 1:2], in_=warm[:, 0:1], func=ACT.Ln)
+        pages = [keep.tile([P, T2], F32, name=f"page{u}") for u in range(PAGES)]
+        for page in pages:
+            nc.gpsimd.memset(page[:], 0.0)
+        w4_s = keep.tile([P, N], U8, name="w4_s", align_bytes=64)
+        nc.gpsimd.memset(w4_s[:].bitcast(I32), 0)
+
+        picked_s = keep.tile([P, S], U8, name="picked_s", tag="picked", align_bytes=64)
         nc.vector.tensor_copy(out=picked_s[:], in_=tab_s[:].indirect(pick[:]))
         for q in range(P // QUAD):
-            nc.gpsimd.dma_start(
+            nc.scalar.dma_start(
                 out=v_s[QUAD * q : QUAD * q + 4, :].bitcast(I32),
                 in_=picked_s[8 * q : 8 * q + 8, :].bitcast(I32),
             )
-
         v_first = keep.tile([P, S], U32, name="v_first", align_bytes=64)
         nc.vector.tensor_copy(out=v_first[:], in_=tab_w[0][:].bitcast(U32).indirect(pick[:]))
 
         w1_c = [keep.tile([P, H], U32, name=f"w1_c{a}", align_bytes=64) for a in range(PASSES)]
         w1_s = [keep.tile([P, H], U8, name=f"w1_s{a}", align_bytes=64) for a in range(PASSES)]
         for a in range(PASSES):
-            grouped = ring.tile([P, PACK * H], BF16, name="grouped", align_bytes=64)
+            grouped = keep.tile([P, PACK * H], BF16, name=f"grouped{a}", tag=f"grouped{a}", align_bytes=64)
             nc.vector.tensor_copy(
                 out=grouped[:].rearrange("p (t m j) -> p m j t", t=PACK, j=PACK),
                 in_=w1_raw[a][:].rearrange("p j (m t) -> p m j t", t=PACK),
@@ -117,30 +98,43 @@ def tile_list_speech_noise_suppression_kernel(
                 in_=tab_w[1][:].bitcast(U32).indirect(pick[:, b * cols_per_half : (b + 1) * cols_per_half]),
             )
 
+        wgs_rows = wgs.rearrange("(p t) j -> p (t j)", t=PACK)
+        wg = keep.tile([P, PACK * S], F32, name="wg", tag="table0", align_bytes=64)
+        for cols in (slice(0, S), slice(S, PACK * S)):
+            for q in (0, 2, 1, 3):
+                nc.sync.dma_start(out=wg[QUAD * q : QUAD * (q + 1), cols], in_=wgs_rows[:, cols])
+        w4_w = keep.tile([P, 2 * N], U8, name="w4_w", tag="picked", align_bytes=64)
+        nc.sync.dma_start(out=w4_w[:].bitcast(I32), in_=w4_words[0].bitcast(I32))
+        for q in range(P // QUAD):
+            nc.sync.dma_start(
+                out=w4_s[QUAD * q : QUAD * q + 4, :].bitcast(I32),
+                in_=w4_scales[0, 4 * q : 4 * q + 4, :].bitcast(I32),
+            )
+        base_rows = base.rearrange("(p t) c -> p t c", t=PACK)
+        starts = [sum(CHUNKS[:i]) for i in range(len(CHUNKS))]
+        base_sb = []
+        for i, (w, tag) in enumerate(zip(BASE_LOADS, ("grouped0", "raw0", "raw1", "table1", "grouped1"))):
+            align = {} if tag.startswith("raw") else {"align_bytes": 64}
+            tile = keep.tile([P, PACK, w], F32, name=f"base{i}", tag=tag, **align)
+            c0 = sum(BASE_LOADS[:i])
+            nc.sync.dma_start(out=tile[:], in_=base_rows[:, :, c0 : c0 + w])
+            base_sb.extend(tile[:, :, c : c + CHUNKS[0]] for c in range(0, w, CHUNKS[0]))
+
         y = {}
         for t in range(PACK):
             for b in range(HALVES):
                 y[t, b] = psum.tile([P, BANK], F32, name="bank")
-                nc.tensor.matmul_mx(
-                    out=y[t, b][:],
-                    lhsT=w1_c[0][:, t * P : (t + 1) * P].bitcast(FP8X4),
-                    lhsT_scale=w1_s[0][:, t * P : (t + 1) * P],
-                    rhs=v_first[:, b * BANK : (b + 1) * BANK].bitcast(FP8X4),
-                    rhs_scale=v_s[:, b * BANK : (b + 1) * BANK],
-                    start=True,
-                    stop=False,
-                )
-        for t in range(PACK):
-            for b in range(HALVES):
-                nc.tensor.matmul_mx(
-                    out=y[t, b][:],
-                    lhsT=w1_c[1][:, t * P : (t + 1) * P].bitcast(FP8X4),
-                    lhsT_scale=w1_s[1][:, t * P : (t + 1) * P],
-                    rhs=v_last[b][:].bitcast(FP8X4),
-                    rhs_scale=v_s[:, S + b * BANK : S + (b + 1) * BANK],
-                    start=False,
-                    stop=True,
-                )
+                moving = (v_first[:, b * BANK : (b + 1) * BANK], v_last[b][:])
+                for a in range(PASSES):
+                    nc.tensor.matmul_mx(
+                        out=y[t, b][:],
+                        lhsT=w1_c[a][:, t * P : (t + 1) * P].bitcast(FP8X4),
+                        lhsT_scale=w1_s[a][:, t * P : (t + 1) * P],
+                        rhs=moving[a].bitcast(FP8X4),
+                        rhs_scale=v_s[:, a * S + b * BANK : a * S + (b + 1) * BANK],
+                        start=a == 0,
+                        stop=a == PASSES - 1,
+                    )
 
         h = [keep.tile([P, S], F32, name=f"h{t}") for t in range(PACK)]
         pieces = [FIRST_PIECES] + [(BANK,) * HALVES] * (PACK - 1)
@@ -155,13 +149,12 @@ def tile_list_speech_noise_suppression_kernel(
         gain = [keep.tile([P, PACK, w], F32, name=f"gain{i}") for i, w in enumerate(CHUNKS)]
         for t in range(PACK):
             page = pages[t % PAGES]
-            weights = wg_first[:] if t == 0 else wg_rest[:, t - 1, :]
             j0 = 0
             for w in FIRST_PIECES if t == 0 else (S,):
                 nc.vector.tensor_tensor(
                     out=page[:].indirect(place[:, j0 // PER_COL : (j0 + w) // PER_COL]),
                     in0=h[t][:, j0 : j0 + w],
-                    in1=weights[:, j0 : j0 + w],
+                    in1=wg[:, t * S + j0 : t * S + j0 + w],
                     op=MULT,
                 )
                 j0 += w
@@ -176,7 +169,7 @@ def tile_list_speech_noise_suppression_kernel(
             nc.vector.tensor_tensor(
                 out=z[:].rearrange("p (c e t) -> p c t e", e=4, t=PACK),
                 in0=gain[i][:].rearrange("p t (c e) -> p c t e", e=4),
-                in1=base_sb[i][:].rearrange("p t (c e) -> p c t e", e=4),
+                in1=base_sb[i].rearrange("p t (c e) -> p c t e", e=4),
                 op=MULT,
             )
             z_c = ring.tile([P, w], U32, name="z_c", align_bytes=64)

@@ -24,8 +24,8 @@ BANK = 512
 HALVES = S // BANK
 PER_COL = 16
 PAGES = 3
-CHUNKS = (256,) * 8
-BASE_LOADS = (256, 512, 512, 512, 256)
+CHUNKS = (128,) + (256,) * 7 + (128,)
+BASE_LOADS = (2, 2, 2, 2, 1)
 FIRST_PIECES = (256, 256, 512)
 
 
@@ -39,21 +39,20 @@ def tile_list_speech_noise_suppression_kernel(
         stage = ctx.enter_context(tc.tile_pool(name="stage", bufs=16))
         psum = ctx.enter_context(tc.psum_pool(name="psum", bufs=8))
 
-        tab_s = keep.tile([P, T], U8, name="tab_s", align_bytes=64)
+        tab_s = keep.tile([P, T], U8, name="tab_s", tag="table1", align_bytes=64)
         nc.sync.dma_start(
             out=tab_s[0:QUAD, :].bitcast(I32), in_=tab_scales.rearrange("a q t -> q a t").bitcast(I32)
         )
         pick = keep.tile([P, S // PER_COL], U16, name="pick")
         nc.sync.dma_start(pick[:], offs)
-        tab_w = [keep.tile([P, T], I32, name=f"tab_w{a}", tag=f"table{a}", align_bytes=64) for a in range(PASSES)]
+        tab_w = [keep.tile([P, T], I32, name="tab_w0", tag="table0", align_bytes=64)]
         nc.sync.dma_start(out=tab_w[0][:], in_=tab_words[0].rearrange("p n i -> p (n i)").bitcast(I32))
-        w1_raw = [keep.tile([P, PACK, H], F32, name=f"w1_raw{a}", tag=f"raw{a}") for a in range(PASSES)]
+        w1_raw = [keep.tile([P, PACK, H], F32, name=f"w1_raw{a}", tag=f"raw{a}", align_bytes=64) for a in range(PASSES)]
         for a in range(PASSES):
             nc.sync.dma_start(
                 out=w1_raw[a][:],
                 in_=w1[a * P * PACK : (a + 1) * P * PACK, :].rearrange("(p j) c -> p j c", j=PACK),
             )
-        nc.sync.dma_start(out=tab_w[1][:], in_=tab_words[1].rearrange("p n i -> p (n i)").bitcast(I32))
         place = keep.tile([P, S // PER_COL], U16, name="place")
         nc.sync.dma_start(place[:], offs2)
 
@@ -73,10 +72,12 @@ def tile_list_speech_noise_suppression_kernel(
         picked_s = keep.tile([P, S], U8, name="picked_s", tag="picked", align_bytes=64)
         nc.vector.tensor_copy(out=picked_s[:], in_=tab_s[:].indirect(pick[:]))
         for q in range(P // QUAD):
-            nc.scalar.dma_start(
+            nc.sync.dma_start(
                 out=v_s[QUAD * q : QUAD * q + 4, :].bitcast(I32),
                 in_=picked_s[8 * q : 8 * q + 8, :].bitcast(I32),
             )
+        tab_w.append(keep.tile([P, T], I32, name="tab_w1", tag="table1", align_bytes=64))
+        nc.sync.dma_start(out=tab_w[1][:], in_=tab_words[1].rearrange("p n i -> p (n i)").bitcast(I32))
         v_first = keep.tile([P, S], U32, name="v_first", align_bytes=64)
         nc.vector.tensor_copy(out=v_first[:], in_=tab_w[0][:].bitcast(U32).indirect(pick[:]))
 
@@ -113,36 +114,39 @@ def tile_list_speech_noise_suppression_kernel(
         base_rows = base.rearrange("(p t) c -> p t c", t=PACK)
         starts = [sum(CHUNKS[:i]) for i in range(len(CHUNKS))]
         base_sb = []
-        for i, (w, tag) in enumerate(zip(BASE_LOADS, ("grouped0", "raw0", "raw1", "table1", "grouped1"))):
-            align = {} if tag.startswith("raw") else {"align_bytes": 64}
-            tile = keep.tile([P, PACK, w], F32, name=f"base{i}", tag=tag, **align)
-            c0 = sum(BASE_LOADS[:i])
-            nc.sync.dma_start(out=tile[:], in_=base_rows[:, :, c0 : c0 + w])
-            base_sb.extend(tile[:, :, c : c + CHUNKS[0]] for c in range(0, w, CHUNKS[0]))
+        for count, tag in zip(BASE_LOADS, ("grouped0", "raw0", "raw1", "table1", "grouped1")):
+            mine = range(len(base_sb), len(base_sb) + count)
+            c0 = starts[mine[0]]
+            width = sum(CHUNKS[i] for i in mine)
+            tile = keep.tile([P, PACK, width], F32, name=f"base{c0}", tag=tag, align_bytes=64)
+            nc.sync.dma_start(out=tile[:], in_=base_rows[:, :, c0 : c0 + width])
+            base_sb.extend([tile[:, :, starts[i] - c0 : starts[i] - c0 + CHUNKS[i]] for i in mine])
 
-        y = {}
-        for t in range(PACK):
-            for b in range(HALVES):
-                y[t, b] = psum.tile([P, BANK], F32, name="bank")
-                moving = (v_first[:, b * BANK : (b + 1) * BANK], v_last[b][:])
-                for a in range(PASSES):
-                    nc.tensor.matmul_mx(
-                        out=y[t, b][:],
-                        lhsT=w1_c[a][:, t * P : (t + 1) * P].bitcast(FP8X4),
-                        lhsT_scale=w1_s[a][:, t * P : (t + 1) * P],
-                        rhs=moving[a].bitcast(FP8X4),
-                        rhs_scale=v_s[:, a * S + b * BANK : a * S + (b + 1) * BANK],
-                        start=a == 0,
-                        stop=a == PASSES - 1,
-                    )
-
-        h = [keep.tile([P, S], F32, name=f"h{t}") for t in range(PACK)]
         pieces = [FIRST_PIECES] + [(BANK,) * HALVES] * (PACK - 1)
+        y = {}
         for t in range(PACK):
             j0 = 0
             for w in pieces[t]:
                 b, c0 = divmod(j0, BANK)
-                nc.scalar.activation(out=h[t][:, j0 : j0 + w], in_=y[t, b][:, c0 : c0 + w], func=ACT.Abs)
+                y[t, j0] = psum.tile([P, BANK], F32, name="bank")
+                moving = (v_first[:, j0 : j0 + w], v_last[b][:, c0 : c0 + w])
+                for a in range(PASSES):
+                    nc.tensor.matmul_mx(
+                        out=y[t, j0][:, 0:w],
+                        lhsT=w1_c[a][:, t * P : (t + 1) * P].bitcast(FP8X4),
+                        lhsT_scale=w1_s[a][:, t * P : (t + 1) * P],
+                        rhs=moving[a].bitcast(FP8X4),
+                        rhs_scale=v_s[:, a * S + j0 : a * S + j0 + w],
+                        start=a == 0,
+                        stop=a == PASSES - 1,
+                    )
+                j0 += w
+
+        h = [keep.tile([P, S], F32, name=f"h{t}") for t in range(PACK)]
+        for t in range(PACK):
+            j0 = 0
+            for w in pieces[t]:
+                nc.scalar.activation(out=h[t][:, j0 : j0 + w], in_=y[t, j0][:, 0:w], func=ACT.Abs)
                 nc.scalar.activation(out=h[t][:, j0 : j0 + w], in_=h[t][:, j0 : j0 + w], func=ACT.Ln, bias=1.0)
                 j0 += w
 
@@ -167,15 +171,15 @@ def tile_list_speech_noise_suppression_kernel(
         for i, w in enumerate(CHUNKS):
             z = ring.tile([P, PACK * w], BF16, name="z", align_bytes=64)
             nc.vector.tensor_tensor(
-                out=z[:].rearrange("p (c e t) -> p c t e", e=4, t=PACK),
-                in0=gain[i][:].rearrange("p t (c e) -> p c t e", e=4),
-                in1=base_sb[i].rearrange("p t (c e) -> p c t e", e=4),
+                out=z[:].rearrange("p (c e t) -> p c t e", e=2, t=PACK),
+                in0=gain[i][:].rearrange("p t (c e) -> p c t e", e=2),
+                in1=base_sb[i].rearrange("p t (c e) -> p c t e", e=2),
                 op=MULT,
             )
             z_c = ring.tile([P, w], U32, name="z_c", align_bytes=64)
             z_s = ring.tile([P, w], U8, name="z_s", align_bytes=64)
             nc.vector.quantize_mx(out=z_c[:].bitcast(FP8X4), scales=z_s[:], in_=z[:])
-            per_bank = BANK // w
+            per_bank = 2
             for g0 in range(0, N // P, per_bank):
                 acc = psum.tile([P, BANK], F32, name="bank")
                 for g in range(g0, g0 + per_bank):
@@ -188,11 +192,11 @@ def tile_list_speech_noise_suppression_kernel(
                         start=True,
                         stop=True,
                     )
-                res = stage.tile([P, BANK], F32, name="res")
-                if i == len(CHUNKS) - 1 and g0 == 0:
-                    nc.vector.tensor_copy(out=res[:], in_=acc[:])
+                res = stage.tile([P, per_bank * w], F32, name="res")
+                if i == len(CHUNKS) - 1:
+                    nc.vector.tensor_copy(out=res[:], in_=acc[:, 0 : per_bank * w])
                 else:
-                    nc.scalar.copy(out=res[:], in_=acc[:])
+                    nc.scalar.copy(out=res[:], in_=acc[:, 0 : per_bank * w])
                 nc.sync.dma_start(
                     out=out_rows[:, g0 : g0 + per_bank, starts[i] : starts[i] + w],
                     in_=res[:].rearrange("p (g c) -> p g c", g=per_bank),

@@ -26,7 +26,11 @@ PER_COL = 16
 PAGES = 3
 CHUNKS = (128,) + (256,) * 7 + (128,)
 BASE_LOADS = (2, 2, 2, 2, 1)
-FIRST_PIECES = (256, 256, 512)
+PIECES = ((0, 0, 256), (1, 0, 512), (0, 256, 256), (0, 512, 512), (1, 512, 512)) + tuple(
+    (t, j0, BANK) for t in (2, 3) for j0 in (0, BANK)
+)
+SCATTERS = ((0, 0, 256), (1, 0, 512), (0, 256, 768), (1, 512, 512), (2, 0, S), (3, 0, S))
+AHEAD = 3
 
 
 def tile_list_speech_noise_suppression_kernel(
@@ -35,7 +39,7 @@ def tile_list_speech_noise_suppression_kernel(
     nc = tc.nc
     with ExitStack() as ctx:
         keep = ctx.enter_context(tc.tile_pool(name="keep", bufs=1))
-        ring = ctx.enter_context(tc.tile_pool(name="ring", bufs=2))
+        ring = ctx.enter_context(tc.tile_pool(name="ring", bufs=3))
         stage = ctx.enter_context(tc.tile_pool(name="stage", bufs=16))
         psum = ctx.enter_context(tc.psum_pool(name="psum", bufs=8))
 
@@ -99,11 +103,11 @@ def tile_list_speech_noise_suppression_kernel(
                 in_=tab_w[1][:].bitcast(U32).indirect(pick[:, b * cols_per_half : (b + 1) * cols_per_half]),
             )
 
-        wgs_rows = wgs.rearrange("(p t) j -> p (t j)", t=PACK)
-        wg = keep.tile([P, PACK * S], F32, name="wg", tag="table0", align_bytes=64)
-        for cols in (slice(0, S), slice(S, PACK * S)):
+        wgs_rows = wgs.rearrange("(p t) j -> p t j", t=PACK)
+        wg = keep.tile([P, PACK, S], F32, name="wg", tag="table0", align_bytes=64)
+        for ts, cols in ((slice(0, 2), slice(0, BANK)), (slice(0, 2), slice(BANK, S)), (slice(2, 4), slice(0, S))):
             for q in (0, 2, 1, 3):
-                nc.sync.dma_start(out=wg[QUAD * q : QUAD * (q + 1), cols], in_=wgs_rows[:, cols])
+                nc.sync.dma_start(out=wg[QUAD * q : QUAD * (q + 1), ts, cols], in_=wgs_rows[:, ts, cols])
         w4_w = keep.tile([P, 2 * N], U8, name="w4_w", tag="picked", align_bytes=64)
         nc.sync.dma_start(out=w4_w[:].bitcast(I32), in_=w4_words[0].bitcast(I32))
         for q in range(P // QUAD):
@@ -122,50 +126,47 @@ def tile_list_speech_noise_suppression_kernel(
             nc.sync.dma_start(out=tile[:], in_=base_rows[:, :, c0 : c0 + width])
             base_sb.extend([tile[:, :, starts[i] - c0 : starts[i] - c0 + CHUNKS[i]] for i in mine])
 
-        pieces = [FIRST_PIECES] + [(BANK,) * HALVES] * (PACK - 1)
         y = {}
-        for t in range(PACK):
-            j0 = 0
-            for w in pieces[t]:
-                b, c0 = divmod(j0, BANK)
-                y[t, j0] = psum.tile([P, BANK], F32, name="bank")
-                moving = (v_first[:, j0 : j0 + w], v_last[b][:, c0 : c0 + w])
-                for a in range(PASSES):
-                    nc.tensor.matmul_mx(
-                        out=y[t, j0][:, 0:w],
-                        lhsT=w1_c[a][:, t * P : (t + 1) * P].bitcast(FP8X4),
-                        lhsT_scale=w1_s[a][:, t * P : (t + 1) * P],
-                        rhs=moving[a].bitcast(FP8X4),
-                        rhs_scale=v_s[:, a * S + j0 : a * S + j0 + w],
-                        start=a == 0,
-                        stop=a == PASSES - 1,
-                    )
-                j0 += w
+        for t, j0, w in PIECES:
+            b, c0 = divmod(j0, BANK)
+            y[t, j0] = psum.tile([P, BANK], F32, name="bank")
+            moving = (v_first[:, j0 : j0 + w], v_last[b][:, c0 : c0 + w])
+            for a in range(PASSES):
+                nc.tensor.matmul_mx(
+                    out=y[t, j0][:, 0:w],
+                    lhsT=w1_c[a][:, t * P : (t + 1) * P].bitcast(FP8X4),
+                    lhsT_scale=w1_s[a][:, t * P : (t + 1) * P],
+                    rhs=moving[a].bitcast(FP8X4),
+                    rhs_scale=v_s[:, a * S + j0 : a * S + j0 + w],
+                    start=a == 0,
+                    stop=a == PASSES - 1,
+                )
 
         h = [keep.tile([P, S], F32, name=f"h{t}") for t in range(PACK)]
-        for t in range(PACK):
-            j0 = 0
-            for w in pieces[t]:
-                nc.scalar.activation(out=h[t][:, j0 : j0 + w], in_=y[t, j0][:, 0:w], func=ACT.Abs)
-                nc.scalar.activation(out=h[t][:, j0 : j0 + w], in_=h[t][:, j0 : j0 + w], func=ACT.Ln, bias=1.0)
-                j0 += w
+        for t, j0, w in PIECES:
+            nc.scalar.activation(out=h[t][:, j0 : j0 + w], in_=y[t, j0][:, 0:w], func=ACT.Abs)
+            nc.scalar.activation(out=h[t][:, j0 : j0 + w], in_=h[t][:, j0 : j0 + w], func=ACT.Ln, bias=1.0)
 
         gain = [keep.tile([P, PACK, w], F32, name=f"gain{i}") for i, w in enumerate(CHUNKS)]
-        for t in range(PACK):
-            page = pages[t % PAGES]
-            j0 = 0
-            for w in FIRST_PIECES if t == 0 else (S,):
-                nc.vector.tensor_tensor(
-                    out=page[:].indirect(place[:, j0 // PER_COL : (j0 + w) // PER_COL]),
-                    in0=h[t][:, j0 : j0 + w],
-                    in1=wg[:, t * S + j0 : t * S + j0 + w],
-                    op=MULT,
-                )
-                j0 += w
-            for i, w in enumerate(CHUNKS):
-                nc.scalar.activation(
-                    out=gain[i][:, t, :], in_=page[:, starts[i] : starts[i] + w], func=ACT.Exp, scale=-1.0
-                )
+
+        def make_gain(t, i):
+            nc.scalar.activation(
+                out=gain[i][:, t, :],
+                in_=pages[t % PAGES][:, starts[i] : starts[i] + CHUNKS[i]],
+                func=ACT.Exp,
+                scale=-1.0,
+            )
+
+        for t, j0, w in SCATTERS:
+            nc.vector.tensor_tensor(
+                out=pages[t % PAGES][:].indirect(place[:, j0 // PER_COL : (j0 + w) // PER_COL]),
+                in0=h[t][:, j0 : j0 + w],
+                in1=wg[:, t, j0 : j0 + w],
+                op=MULT,
+            )
+            if j0 + w == S:
+                for i in range(len(CHUNKS) if t < PACK - 1 else AHEAD):
+                    make_gain(t, i)
 
         out_rows = out.rearrange("(g p) c -> p g c", p=P)
         for i, w in enumerate(CHUNKS):
@@ -201,3 +202,5 @@ def tile_list_speech_noise_suppression_kernel(
                     out=out_rows[:, g0 : g0 + per_bank, starts[i] : starts[i] + w],
                     in_=res[:].rearrange("p (g c) -> p g c", g=per_bank),
                 )
+            if i + AHEAD < len(CHUNKS):
+                make_gain(PACK - 1, i + AHEAD)

@@ -43,12 +43,14 @@ def tile_list_speech_noise_suppression_kernel(
         stage = ctx.enter_context(tc.tile_pool(name="stage", bufs=16))
         psum = ctx.enter_context(tc.psum_pool(name="psum", bufs=8))
 
-        tab_s = keep.tile([P, T], U8, name="tab_s", tag="table1", align_bytes=64)
+        tab_s = keep.tile([P, T], U8, name="tab_s", align_bytes=64)
         nc.sync.dma_start(
             out=tab_s[0:QUAD, :].bitcast(I32), in_=tab_scales.rearrange("a q t -> q a t").bitcast(I32)
         )
         pick = keep.tile([P, S // PER_COL], U16, name="pick")
         nc.sync.dma_start(pick[:], offs)
+        place = keep.tile([P, S // PER_COL], U16, name="place")
+        nc.sync.dma_start(place[:], offs2)
         tab_w = [keep.tile([P, T], I32, name="tab_w0", tag="table0", align_bytes=64)]
         nc.sync.dma_start(out=tab_w[0][:], in_=tab_words[0].rearrange("p n i -> p (n i)").bitcast(I32))
         w1_raw = [keep.tile([P, PACK, H], F32, name=f"w1_raw{a}", tag=f"raw{a}", align_bytes=64) for a in range(PASSES)]
@@ -57,8 +59,8 @@ def tile_list_speech_noise_suppression_kernel(
                 out=w1_raw[a][:],
                 in_=w1[a * P * PACK : (a + 1) * P * PACK, :].rearrange("(p j) c -> p j c", j=PACK),
             )
-        place = keep.tile([P, S // PER_COL], U16, name="place")
-        nc.sync.dma_start(place[:], offs2)
+        tab_w.append(keep.tile([P, T], I32, name="tab_w1", tag="table1", align_bytes=64))
+        nc.sync.dma_start(out=tab_w[1][:], in_=tab_words[1].rearrange("p n i -> p (n i)").bitcast(I32))
 
         nc.gpsimd.memset(tab_s[QUAD : 2 * QUAD, :].bitcast(I32), 0)
         nc.gpsimd.memset(tab_s[2 * QUAD : P, :].bitcast(I32), 0)
@@ -80,8 +82,6 @@ def tile_list_speech_noise_suppression_kernel(
                 out=v_s[QUAD * q : QUAD * q + 4, :].bitcast(I32),
                 in_=picked_s[8 * q : 8 * q + 8, :].bitcast(I32),
             )
-        tab_w.append(keep.tile([P, T], I32, name="tab_w1", tag="table1", align_bytes=64))
-        nc.sync.dma_start(out=tab_w[1][:], in_=tab_words[1].rearrange("p n i -> p (n i)").bitcast(I32))
         v_first = keep.tile([P, S], U32, name="v_first", align_bytes=64)
         nc.vector.tensor_copy(out=v_first[:], in_=tab_w[0][:].bitcast(U32).indirect(pick[:]))
 
@@ -89,7 +89,7 @@ def tile_list_speech_noise_suppression_kernel(
         w1_s = [keep.tile([P, H], U8, name=f"w1_s{a}", align_bytes=64) for a in range(PASSES)]
         for a in range(PASSES):
             grouped = keep.tile([P, PACK * H], BF16, name=f"grouped{a}", tag=f"grouped{a}", align_bytes=64)
-            nc.vector.tensor_copy(
+            (nc.scalar.copy if a == 0 else nc.vector.tensor_copy)(
                 out=grouped[:].rearrange("p (t m j) -> p m j t", t=PACK, j=PACK),
                 in_=w1_raw[a][:].rearrange("p j (m t) -> p m j t", t=PACK),
             )
@@ -105,9 +105,11 @@ def tile_list_speech_noise_suppression_kernel(
 
         wgs_rows = wgs.rearrange("(p t) j -> p t j", t=PACK)
         wg = keep.tile([P, PACK, S], F32, name="wg", tag="table0", align_bytes=64)
-        for ts, cols in ((slice(0, 2), slice(0, BANK)), (slice(0, 2), slice(BANK, S)), (slice(2, 4), slice(0, S))):
+        for t, j0, w in SCATTERS:
             for q in (0, 2, 1, 3):
-                nc.sync.dma_start(out=wg[QUAD * q : QUAD * (q + 1), ts, cols], in_=wgs_rows[:, ts, cols])
+                nc.sync.dma_start(
+                    out=wg[QUAD * q : QUAD * (q + 1), t, j0 : j0 + w], in_=wgs_rows[:, t, j0 : j0 + w]
+                )
         w4_w = keep.tile([P, 2 * N], U8, name="w4_w", tag="picked", align_bytes=64)
         nc.sync.dma_start(out=w4_w[:].bitcast(I32), in_=w4_words[0].bitcast(I32))
         for q in range(P // QUAD):

@@ -31,6 +31,7 @@ PIECES = ((0, 0, 256), (1, 0, 512), (0, 256, 256), (0, 512, 512), (1, 512, 512))
 )
 SCATTERS = ((0, 0, 256), (1, 0, 512), (0, 256, 768), (1, 512, 512), (2, 0, S), (3, 0, S))
 AHEAD = 3
+FILL = 64
 
 
 def tile_list_speech_noise_suppression_kernel(
@@ -49,8 +50,6 @@ def tile_list_speech_noise_suppression_kernel(
         )
         pick = keep.tile([P, S // PER_COL], U16, name="pick")
         nc.sync.dma_start(pick[:], offs)
-        place = keep.tile([P, S // PER_COL], U16, name="place")
-        nc.sync.dma_start(place[:], offs2)
         tab_w = [keep.tile([P, T], I32, name="tab_w0", tag="table0", align_bytes=64)]
         nc.sync.dma_start(out=tab_w[0][:], in_=tab_words[0].rearrange("p n i -> p (n i)").bitcast(I32))
         w1_raw = [keep.tile([P, PACK, H], F32, name=f"w1_raw{a}", tag=f"raw{a}", align_bytes=64) for a in range(PASSES)]
@@ -61,6 +60,9 @@ def tile_list_speech_noise_suppression_kernel(
             )
         tab_w.append(keep.tile([P, T], I32, name="tab_w1", tag="table1", align_bytes=64))
         nc.sync.dma_start(out=tab_w[1][:], in_=tab_words[1].rearrange("p n i -> p (n i)").bitcast(I32))
+
+        place = keep.tile([P, S // PER_COL], U16, name="place")
+        nc.sync.dma_start(place[:], offs2)
 
         nc.gpsimd.memset(tab_s[QUAD : 2 * QUAD, :].bitcast(I32), 0)
         nc.gpsimd.memset(tab_s[2 * QUAD : P, :].bitcast(I32), 0)
@@ -77,7 +79,7 @@ def tile_list_speech_noise_suppression_kernel(
 
         picked_s = keep.tile([P, S], U8, name="picked_s", tag="picked", align_bytes=64)
         nc.vector.tensor_copy(out=picked_s[:], in_=tab_s[:].indirect(pick[:]))
-        for q in range(P // QUAD):
+        for q in (0, 2, 1, 3):
             nc.sync.dma_start(
                 out=v_s[QUAD * q : QUAD * q + 4, :].bitcast(I32),
                 in_=picked_s[8 * q : 8 * q + 8, :].bitcast(I32),
@@ -133,15 +135,16 @@ def tile_list_speech_noise_suppression_kernel(
             b, c0 = divmod(j0, BANK)
             y[t, j0] = psum.tile([P, BANK], F32, name="bank")
             moving = (v_first[:, j0 : j0 + w], v_last[b][:, c0 : c0 + w])
-            for a in range(PASSES):
+            order = (0, 1) if (t, j0) == (0, 0) else (1, 0)
+            for a in order:
                 nc.tensor.matmul_mx(
                     out=y[t, j0][:, 0:w],
                     lhsT=w1_c[a][:, t * P : (t + 1) * P].bitcast(FP8X4),
                     lhsT_scale=w1_s[a][:, t * P : (t + 1) * P],
                     rhs=moving[a].bitcast(FP8X4),
                     rhs_scale=v_s[:, a * S + j0 : a * S + j0 + w],
-                    start=a == 0,
-                    stop=a == PASSES - 1,
+                    start=a == order[0],
+                    stop=a == order[1],
                 )
 
         h = [keep.tile([P, S], F32, name=f"h{t}") for t in range(PACK)]
@@ -173,12 +176,13 @@ def tile_list_speech_noise_suppression_kernel(
         out_rows = out.rearrange("(g p) c -> p g c", p=P)
         for i, w in enumerate(CHUNKS):
             z = ring.tile([P, PACK * w], BF16, name="z", align_bytes=64)
-            nc.vector.tensor_tensor(
-                out=z[:].rearrange("p (c e t) -> p c t e", e=2, t=PACK),
-                in0=gain[i][:].rearrange("p t (c e) -> p c t e", e=2),
-                in1=base_sb[i].rearrange("p t (c e) -> p c t e", e=2),
-                op=MULT,
-            )
+            for c0, c1 in ((0, w),) if i not in (1, 6, 7, 8) else ((0, FILL), (FILL, w)):
+                nc.vector.tensor_tensor(
+                    out=z[:, PACK * c0 : PACK * c1].rearrange("p (c e t) -> p c t e", e=2, t=PACK),
+                    in0=gain[i][:, :, c0:c1].rearrange("p t (c e) -> p c t e", e=2),
+                    in1=base_sb[i][:, :, c0:c1].rearrange("p t (c e) -> p c t e", e=2),
+                    op=MULT,
+                )
             z_c = ring.tile([P, w], U32, name="z_c", align_bytes=64)
             z_s = ring.tile([P, w], U8, name="z_s", align_bytes=64)
             nc.vector.quantize_mx(out=z_c[:].bitcast(FP8X4), scales=z_s[:], in_=z[:])
@@ -196,7 +200,7 @@ def tile_list_speech_noise_suppression_kernel(
                         stop=True,
                     )
                 res = stage.tile([P, per_bank * w], F32, name="res")
-                if i == len(CHUNKS) - 1:
+                if i >= len(CHUNKS) - 2 and (g0 > 0) == (i < len(CHUNKS) - 1):
                     nc.vector.tensor_copy(out=res[:], in_=acc[:, 0 : per_bank * w])
                 else:
                     nc.scalar.copy(out=res[:], in_=acc[:, 0 : per_bank * w])

@@ -176,7 +176,7 @@ def tile_list_speech_noise_suppression_kernel(
         out_rows = out.rearrange("(g p) c -> p g c", p=P)
         for i, w in enumerate(CHUNKS):
             z = ring.tile([P, PACK * w], BF16, name="z", align_bytes=64)
-            for c0, c1 in ((0, w),) if i not in (1, 6, 7, 8) else ((0, FILL), (FILL, w)):
+            for c0, c1 in ((0, w),) if i == 0 else ((0, FILL), (FILL, w)):
                 nc.vector.tensor_tensor(
                     out=z[:, PACK * c0 : PACK * c1].rearrange("p (c e t) -> p c t e", e=2, t=PACK),
                     in0=gain[i][:, :, c0:c1].rearrange("p t (c e) -> p c t e", e=2),

@@ -19,17 +19,17 @@ MULT = mybir.AluOpType.mult
 P = 128
 PACK = 4
 QUAD = 32
+MID = P // 2
 PASSES = K // (P * PACK)
 BANK = 512
 HALVES = S // BANK
 PER_COL = 16
 PAGES = 3
+KB = 1024
 CHUNKS = (128,) + (256,) * 7 + (128,)
 BASE_LOADS = (2, 2, 2, 2, 1)
-PIECES = ((0, 0, 256), (1, 0, 512), (0, 256, 256), (0, 512, 512), (1, 512, 512)) + tuple(
-    (t, j0, BANK) for t in (2, 3) for j0 in (0, BANK)
-)
-SCATTERS = ((0, 0, 256), (1, 0, 512), (0, 256, 768), (1, 512, 512), (2, 0, S), (3, 0, S))
+GAIN_GROUPS = (1, 2, 2, 2, 2)
+QUARTERS = (0, 2, 1, 3)
 AHEAD = 3
 FILL = 64
 
@@ -40,9 +40,21 @@ def tile_list_speech_noise_suppression_kernel(
     nc = tc.nc
     with ExitStack() as ctx:
         keep = ctx.enter_context(tc.tile_pool(name="keep", bufs=1))
+        placed = ctx.enter_context(tc.tile_pool(name="placed", bufs=1))
         ring = ctx.enter_context(tc.tile_pool(name="ring", bufs=3))
         stage = ctx.enter_context(tc.tile_pool(name="stage", bufs=16))
         psum = ctx.enter_context(tc.psum_pool(name="psum", bufs=8))
+
+        def put(shape, dtype, name, at):
+            return placed.tile(shape, dtype, name=name, offset=at, align_bytes=64)
+
+        def load_w1(tile, a, half):
+            nc.sync.dma_start(
+                out=tile[:],
+                in_=w1[a * P * PACK : (a + 1) * P * PACK, half * H // 2 : (half + 1) * H // 2].rearrange(
+                    "(p j) c -> p j c", j=PACK
+                ),
+            )
 
         tab_s = keep.tile([P, T], U8, name="tab_s", align_bytes=64)
         nc.sync.dma_start(
@@ -50,52 +62,79 @@ def tile_list_speech_noise_suppression_kernel(
         )
         pick = keep.tile([P, S // PER_COL], U16, name="pick")
         nc.sync.dma_start(pick[:], offs)
-        tab_w = [keep.tile([P, T], I32, name="tab_w0", tag="table0", align_bytes=64)]
-        nc.sync.dma_start(out=tab_w[0][:], in_=tab_words[0].rearrange("p n i -> p (n i)").bitcast(I32))
-        w1_raw = [keep.tile([P, PACK, H], F32, name=f"w1_raw{a}", tag=f"raw{a}", align_bytes=64) for a in range(PASSES)]
-        for a in range(PASSES):
-            nc.sync.dma_start(
-                out=w1_raw[a][:],
-                in_=w1[a * P * PACK : (a + 1) * P * PACK, :].rearrange("(p j) c -> p j c", j=PACK),
-            )
-        tab_w.append(keep.tile([P, T], I32, name="tab_w1", tag="table1", align_bytes=64))
-        nc.sync.dma_start(out=tab_w[1][:], in_=tab_words[1].rearrange("p n i -> p (n i)").bitcast(I32))
-
         place = keep.tile([P, S // PER_COL], U16, name="place")
         nc.sync.dma_start(place[:], offs2)
+        tab_w = [put([P, T], I32, "tab_w0", 0), put([P, T], I32, "tab_w1", 52 * KB)]
+        nc.sync.dma_start(out=tab_w[0][:], in_=tab_words[0].rearrange("p n i -> p (n i)").bitcast(I32))
+        raw = {(a, 0): put([P, PACK, H // 2], F32, f"raw_low{a}", (70 + 4 * a) * KB) for a in range(PASSES)}
+        for a in range(PASSES):
+            load_w1(raw[a, 0], a, 0)
+        nc.sync.dma_start(out=tab_w[1][:], in_=tab_words[1].rearrange("p n i -> p (n i)").bitcast(I32))
 
         nc.gpsimd.memset(tab_s[QUAD : 2 * QUAD, :].bitcast(I32), 0)
         nc.gpsimd.memset(tab_s[2 * QUAD : P, :].bitcast(I32), 0)
-        v_s = keep.tile([P, PASSES * S], U8, name="v_s", align_bytes=64)
-        nc.vector.memset(v_s[:].bitcast(I32), 0)
+        v_s = [keep.tile([P, PASSES * BANK], U8, name="v_s0", align_bytes=64), put([P, PASSES * BANK], U8, "v_s1", 12 * KB)]
+        nc.vector.memset(v_s[0][:].bitcast(I32), 0)
         warm = keep.tile([P, 2], F32, name="warm")
         nc.vector.memset(warm[:, 0:1], 1.0)
         nc.scalar.activation(out=warm[:, 1:2], in_=warm[:, 0:1], func=ACT.Ln)
+
+        picked_s = keep.tile([P, S], U8, name="picked_s", tag="picked", align_bytes=64)
+        nc.vector.tensor_copy(out=picked_s[:], in_=tab_s[:].indirect(pick[:]))
+
+        def move_scales(b):
+            for q in QUARTERS:
+                nc.sync.dma_start(
+                    out=v_s[b][QUAD * q : QUAD * q + 4, :].bitcast(I32),
+                    in_=picked_s[8 * q : 8 * q + 8, b * BANK : (b + 1) * BANK].bitcast(I32),
+                )
+
+        move_scales(0)
+        v_first = keep.tile([P, S], U32, name="v_first", align_bytes=64)
+        nc.vector.tensor_copy(out=v_first[:], in_=tab_w[0][:].bitcast(U32).indirect(pick[:]))
+        nc.vector.memset(v_s[1][:].bitcast(I32), 0)
         pages = [keep.tile([P, T2], F32, name=f"page{u}") for u in range(PAGES)]
-        for page in pages:
+        nc.vector.memset(pages[0][:], 0.0)
+        for page in pages[1:]:
             nc.gpsimd.memset(page[:], 0.0)
         w4_s = keep.tile([P, N], U8, name="w4_s", align_bytes=64)
         nc.gpsimd.memset(w4_s[:].bitcast(I32), 0)
 
-        picked_s = keep.tile([P, S], U8, name="picked_s", tag="picked", align_bytes=64)
-        nc.vector.tensor_copy(out=picked_s[:], in_=tab_s[:].indirect(pick[:]))
-        for q in (0, 2, 1, 3):
-            nc.sync.dma_start(
-                out=v_s[QUAD * q : QUAD * q + 4, :].bitcast(I32),
-                in_=picked_s[8 * q : 8 * q + 8, :].bitcast(I32),
-            )
-        v_first = keep.tile([P, S], U32, name="v_first", align_bytes=64)
-        nc.vector.tensor_copy(out=v_first[:], in_=tab_w[0][:].bitcast(U32).indirect(pick[:]))
+        w1_c = {
+            (s, a): keep.tile([P, P], U32, name=f"w1_c{s}{a}", align_bytes=64)
+            for s in range(PACK)
+            for a in range(PASSES)
+            if (s, a) != (1, 1)
+        }
+        w1_c[1, 1] = put([P, P], U32, "w1_c11", 93 * KB)
+        w1_s = [keep.tile([P, PASSES * P], U8, name=f"w1_s{s}", align_bytes=64) for s in range(PACK)]
+        grouped = {}
 
-        w1_c = [keep.tile([P, H], U32, name=f"w1_c{a}", align_bytes=64) for a in range(PASSES)]
-        w1_s = [keep.tile([P, H], U8, name=f"w1_s{a}", align_bytes=64) for a in range(PASSES)]
-        for a in range(PASSES):
-            grouped = keep.tile([P, PACK * H], BF16, name=f"grouped{a}", tag=f"grouped{a}", align_bytes=64)
-            (nc.scalar.copy if a == 0 else nc.vector.tensor_copy)(
-                out=grouped[:].rearrange("p (t m j) -> p m j t", t=PACK, j=PACK),
-                in_=w1_raw[a][:].rearrange("p j (m t) -> p m j t", t=PACK),
+        def cast(a, half, t0, at, copy=nc.scalar.copy):
+            grouped[a, half, t0] = put([P, 2 * MID * PACK], BF16, f"grouped{a}{half}{t0}", at)
+            copy(
+                out=grouped[a, half, t0][:].rearrange("p (t u j) -> p u j t", t=2, j=PACK),
+                in_=raw[a, half][:].rearrange("p j (u t) -> p u j t", t=PACK)[:, :, :, t0 : t0 + 2],
             )
-            nc.vector.quantize_mx(out=w1_c[a][:].bitcast(FP8X4), scales=w1_s[a][:], in_=grouped[:])
+
+        def quantise(a, half, t0):
+            src = grouped[a, half, t0]
+            if t0 == 0:
+                cols = slice(a * P, (a + 1) * P)
+                nc.vector.quantize_mx(out=w1_c[half, a][:].bitcast(FP8X4), scales=w1_s[half][:, cols], in_=src[:])
+            else:
+                cols = slice(a * P + half * MID, a * P + (half + 1) * MID)
+                for t in (2, 3):
+                    nc.vector.quantize_mx(
+                        out=w1_c[t, a][:, half * MID : (half + 1) * MID].bitcast(FP8X4),
+                        scales=w1_s[t][:, cols],
+                        in_=src[:, (t - 2) * MID * PACK : (t - 1) * MID * PACK],
+                    )
+
+        for a in range(PASSES):
+            for t0 in (0, 2):
+                cast(a, 0, t0, (78 + 8 * a + t0 // 2) * KB)
+                quantise(a, 0, t0)
 
         v_last = [keep.tile([P, BANK], U32, name=f"v_last{b}", align_bytes=64) for b in range(HALVES)]
         cols_per_half = BANK // PER_COL
@@ -106,12 +145,21 @@ def tile_list_speech_noise_suppression_kernel(
             )
 
         wgs_rows = wgs.rearrange("(p t) j -> p t j", t=PACK)
-        wg = keep.tile([P, PACK, S], F32, name="wg", tag="table0", align_bytes=64)
-        for t, j0, w in SCATTERS:
-            for q in (0, 2, 1, 3):
-                nc.sync.dma_start(
-                    out=wg[QUAD * q : QUAD * (q + 1), t, j0 : j0 + w], in_=wgs_rows[:, t, j0 : j0 + w]
-                )
+
+        def load_wgs(tile, rows, j0, w):
+            for q in QUARTERS:
+                nc.sync.dma_start(out=tile[QUAD * q : QUAD * (q + 1), :], in_=wgs_rows[:, rows[q // 2], j0 : j0 + w])
+
+        wg_low = put([P, S], F32, "wg_low", 0)
+        for a in range(PASSES):
+            raw[a, 1] = put([P, PACK, H // 2], F32, f"raw_high{a}", (4 + 4 * a) * KB)
+            load_w1(raw[a, 1], a, 1)
+            load_wgs(wg_low[:, BANK * a : BANK * (a + 1)], (0, 1), BANK * a, BANK)
+            if a == 0:
+                move_scales(1)
+        wg_high = {2: put([P, S], F32, "wg2", 13 * KB), 3: put([P, S], F32, "wg3", 52 * KB)}
+        for t in (2, 3):
+            load_wgs(wg_high[t][:], (t, t), 0, S)
         w4_w = keep.tile([P, 2 * N], U8, name="w4_w", tag="picked", align_bytes=64)
         nc.sync.dma_start(out=w4_w[:].bitcast(I32), in_=w4_words[0].bitcast(I32))
         for q in range(P // QUAD):
@@ -122,56 +170,101 @@ def tile_list_speech_noise_suppression_kernel(
         base_rows = base.rearrange("(p t) c -> p t c", t=PACK)
         starts = [sum(CHUNKS[:i]) for i in range(len(CHUNKS))]
         base_sb = []
-        for count, tag in zip(BASE_LOADS, ("grouped0", "raw0", "raw1", "table1", "grouped1")):
+        for count in BASE_LOADS:
             mine = range(len(base_sb), len(base_sb) + count)
             c0 = starts[mine[0]]
             width = sum(CHUNKS[i] for i in mine)
-            tile = keep.tile([P, PACK, width], F32, name=f"base{c0}", tag=tag, align_bytes=64)
+            tile = put([P, PACK, width], F32, f"base{c0}", 56 * KB + 16 * c0)
             nc.sync.dma_start(out=tile[:], in_=base_rows[:, :, c0 : c0 + width])
             base_sb.extend([tile[:, :, starts[i] - c0 : starts[i] - c0 + CHUNKS[i]] for i in mine])
 
-        y = {}
-        for t, j0, w in PIECES:
+        h = {s: keep.tile([P, S], F32, name=f"h{s}") for s in (0, 2, 3)}
+        h_late = put([P, BANK], F32, "h_late", 8 * KB)
+        first_abs = put([P, S], F32, "first_abs", 94 * KB)
+        h[1] = put([P, S], F32, "h1", 95 * KB)
+        h_second = put([P, 256], F32, "h_second", 92 * KB)
+
+        def logs(s, j0, w):
+            return {(0, 256): h_second[:], (0, BANK): h_late[:]}.get((s, j0), h[s][:, j0 : j0 + w])
+
+        last_abs = put([P, PACK * T2], F32, "last_abs", 20 * KB)
+
+        def make_h(s, j0, w):
             b, c0 = divmod(j0, BANK)
-            y[t, j0] = psum.tile([P, BANK], F32, name="bank")
+            y = psum.tile([P, BANK], F32, name="bank")
             moving = (v_first[:, j0 : j0 + w], v_last[b][:, c0 : c0 + w])
-            order = (0, 1) if (t, j0) == (0, 0) else (1, 0)
+            order = (1, 0) if s == 0 and j0 > 0 else (0, 1)
             for a in order:
                 nc.tensor.matmul_mx(
-                    out=y[t, j0][:, 0:w],
-                    lhsT=w1_c[a][:, t * P : (t + 1) * P].bitcast(FP8X4),
-                    lhsT_scale=w1_s[a][:, t * P : (t + 1) * P],
+                    out=y[:, 0:w],
+                    lhsT=w1_c[s, a][:].bitcast(FP8X4),
+                    lhsT_scale=w1_s[s][:, a * P : (a + 1) * P],
                     rhs=moving[a].bitcast(FP8X4),
-                    rhs_scale=v_s[:, a * S + j0 : a * S + j0 + w],
+                    rhs_scale=v_s[b][:, a * BANK + c0 : a * BANK + c0 + w],
                     start=a == order[0],
                     stop=a == order[1],
                 )
+            size = first_abs[:, 0:w] if s == 0 else last_abs[:, 0:w] if (s, j0 + w) == (PACK - 1, S) else logs(s, j0, w)
+            nc.scalar.activation(out=size, in_=y[:, 0:w], func=ACT.Abs)
+            nc.scalar.activation(out=logs(s, j0, w), in_=size, func=ACT.Ln, bias=1.0)
 
-        h = [keep.tile([P, S], F32, name=f"h{t}") for t in range(PACK)]
-        for t, j0, w in PIECES:
-            nc.scalar.activation(out=h[t][:, j0 : j0 + w], in_=y[t, j0][:, 0:w], func=ACT.Abs)
-            nc.scalar.activation(out=h[t][:, j0 : j0 + w], in_=h[t][:, j0 : j0 + w], func=ACT.Ln, bias=1.0)
-
-        gain = [keep.tile([P, PACK, w], F32, name=f"gain{i}") for i, w in enumerate(CHUNKS)]
-
-        def make_gain(t, i):
-            nc.scalar.activation(
-                out=gain[i][:, t, :],
-                in_=pages[t % PAGES][:, starts[i] : starts[i] + CHUNKS[i]],
-                func=ACT.Exp,
-                scale=-1.0,
-            )
-
-        for t, j0, w in SCATTERS:
+        def scatter(s, j0, w):
             nc.vector.tensor_tensor(
-                out=pages[t % PAGES][:].indirect(place[:, j0 // PER_COL : (j0 + w) // PER_COL]),
-                in0=h[t][:, j0 : j0 + w],
-                in1=wg[:, t, j0 : j0 + w],
+                out=pages[s % PAGES][:].indirect(place[:, j0 // PER_COL : (j0 + w) // PER_COL]),
+                in0=logs(s, j0, w),
+                in1=(wg_low if s < 2 else wg_high[s])[:, j0 : j0 + w],
                 op=MULT,
             )
-            if j0 + w == S:
-                for i in range(len(CHUNKS) if t < PACK - 1 else AHEAD):
-                    make_gain(t, i)
+
+        cast(0, 1, 0, 88 * KB, copy=nc.vector.tensor_copy)
+        quantise(0, 1, 0)
+        for j0 in (0, 256):
+            make_h(0, j0, 256)
+            scatter(0, j0, 256)
+        cast(1, 1, 2, 91 * KB)
+        cast(1, 1, 0, 89 * KB)
+        quantise(1, 1, 0)
+        make_h(0, BANK, BANK)
+        scatter(0, BANK, BANK)
+        cast(0, 1, 2, 94 * KB)
+        for a in range(PASSES):
+            quantise(a, 1, 2)
+        for s in (1, 2, 3):
+            for j0 in (0, BANK):
+                make_h(s, j0, BANK)
+        for s in (1, 2):
+            scatter(s, 0, S)
+
+        groups = []
+        gain = []
+        for count in GAIN_GROUPS:
+            mine = range(len(gain), len(gain) + count)
+            c0 = starts[mine[0]]
+            width = sum(CHUNKS[i] for i in mine)
+            tile = put([P, PACK, width], F32, f"gain{c0}", 20 * KB + 16 * c0)
+            groups.append((tile, c0, width))
+            gain.extend([tile[:, :, starts[i] - c0 : starts[i] - c0 + CHUNKS[i]] for i in mine])
+
+        def make_gain(dst, src):
+            nc.scalar.activation(out=dst, in_=src, func=ACT.Exp, scale=-1.0)
+
+        for tile, c0, w in groups:
+            make_gain(tile[:, 0, :], pages[0][:, c0 : c0 + w])
+            nc.sync.dma_start(out=tile[0:MID, 1, :], in_=tile[MID:P, 0, :])
+        scatter(3, 0, S)
+        for tile, c0, w in groups:
+            make_gain(tile[0:MID, 3, :], pages[1][0:MID, c0 : c0 + w])
+            nc.sync.dma_start(out=tile[MID:P, 0, :], in_=tile[0:MID, 3, :])
+        for tile, c0, w in groups:
+            make_gain(tile[MID:P, 1, :], pages[1][MID:P, c0 : c0 + w])
+        for tile, c0, w in groups:
+            make_gain(tile[:, 2, :], pages[2][:, c0 : c0 + w])
+
+        def last_gain(i):
+            make_gain(gain[i][:, PACK - 1, :], pages[0][:, starts[i] : starts[i] + CHUNKS[i]])
+
+        for i in range(AHEAD):
+            last_gain(i)
 
         out_rows = out.rearrange("(g p) c -> p g c", p=P)
         for i, w in enumerate(CHUNKS):
@@ -209,4 +302,4 @@ def tile_list_speech_noise_suppression_kernel(
                     in_=res[:].rearrange("p (g c) -> p g c", g=per_bank),
                 )
             if i + AHEAD < len(CHUNKS):
-                make_gain(PACK - 1, i + AHEAD)
+                last_gain(i + AHEAD)

@@ -111,17 +111,26 @@ def tile_list_speech_noise_suppression_kernel(
         grouped = {}
 
         def cast(a, half, t0, at, copy=nc.scalar.copy):
-            grouped[a, half, t0] = put([P, 2 * MID * PACK], BF16, f"grouped{a}{half}{t0}", at)
+            grouped[a, half, t0] = put([P, 2 * MID * PACK], BF16, f"grouped{a}{half}{t0}", at)[:]
             copy(
-                out=grouped[a, half, t0][:].rearrange("p (t u j) -> p u j t", t=2, j=PACK),
+                out=grouped[a, half, t0].rearrange("p (t u j) -> p u j t", t=2, j=PACK),
                 in_=raw[a, half][:].rearrange("p j (u t) -> p u j t", t=PACK)[:, :, :, t0 : t0 + 2],
             )
+
+        def cast_whole(a, half, at):
+            whole = put([P, PACK * MID * PACK], BF16, f"whole{a}{half}", at)
+            nc.scalar.copy(
+                out=whole[:].rearrange("p (t u j) -> p u j t", t=PACK, j=PACK),
+                in_=raw[a, half][:].rearrange("p j (u t) -> p u j t", t=PACK),
+            )
+            for t0 in (0, 2):
+                grouped[a, half, t0] = whole[:, t0 * MID * PACK : (t0 + 2) * MID * PACK]
 
         def quantise(a, half, t0):
             src = grouped[a, half, t0]
             if t0 == 0:
                 cols = slice(a * P, (a + 1) * P)
-                nc.vector.quantize_mx(out=w1_c[half, a][:].bitcast(FP8X4), scales=w1_s[half][:, cols], in_=src[:])
+                nc.vector.quantize_mx(out=w1_c[half, a][:].bitcast(FP8X4), scales=w1_s[half][:, cols], in_=src)
             else:
                 cols = slice(a * P + half * MID, a * P + (half + 1) * MID)
                 for t in (2, 3):
@@ -221,8 +230,7 @@ def tile_list_speech_noise_suppression_kernel(
         for j0 in (0, 256):
             make_h(0, j0, 256)
             scatter(0, j0, 256)
-        cast(1, 1, 2, 91 * KB)
-        cast(1, 1, 0, 89 * KB)
+        cast_whole(1, 1, 89 * KB)
         quantise(1, 1, 0)
         make_h(0, BANK, BANK)
         scatter(0, BANK, BANK)

@@ -22,16 +22,38 @@ QUAD = 32
 MID = P // 2
 PASSES = K // (P * PACK)
 BANK = 512
+BANKS = 8
 HALVES = S // BANK
 PER_COL = 16
 PAGES = 3
-KB = 1024
+PIECE = 256
 CHUNKS = (128,) + (256,) * 7 + (128,)
 BASE_LOADS = (2, 2, 2, 2, 1)
 GAIN_GROUPS = (1, 2, 2, 2, 2)
 QUARTERS = (0, 2, 1, 3)
 AHEAD = 3
 FILL = 64
+GROUPS_PER_BANK = 2
+RING = 3
+STAGES = 16
+
+KB = 1024
+WORD = 4
+AT_TABLE = (0, 52 * KB)
+AT_WGS_LOW = 0
+AT_RAW_HIGH = (4 * KB, 8 * KB)
+AT_LATE_SCALES = 12 * KB
+AT_WGS_HIGH = {2: 13 * KB, 3: 52 * KB}
+AT_LATE_LOGS = AT_RAW_HIGH[1]
+AT_GAIN = 20 * KB
+AT_BASE = 56 * KB
+AT_RAW_LOW = (70 * KB, 74 * KB)
+AT_ROUNDED_LOW = (78 * KB, 86 * KB)
+AT_ROUNDED_HIGH = (88 * KB, 89 * KB)
+AT_SECOND_LOGS = 92 * KB
+AT_LATE_CODES = 93 * KB
+AT_FIRST_ABS = 94 * KB
+AT_SLICE1_LOGS = 95 * KB
 
 
 def tile_list_speech_noise_suppression_kernel(
@@ -41,9 +63,9 @@ def tile_list_speech_noise_suppression_kernel(
     with ExitStack() as ctx:
         keep = ctx.enter_context(tc.tile_pool(name="keep", bufs=1))
         placed = ctx.enter_context(tc.tile_pool(name="placed", bufs=1))
-        ring = ctx.enter_context(tc.tile_pool(name="ring", bufs=3))
-        stage = ctx.enter_context(tc.tile_pool(name="stage", bufs=16))
-        psum = ctx.enter_context(tc.psum_pool(name="psum", bufs=8))
+        ring = ctx.enter_context(tc.tile_pool(name="ring", bufs=RING))
+        stage = ctx.enter_context(tc.tile_pool(name="stage", bufs=STAGES))
+        psum = ctx.enter_context(tc.psum_pool(name="psum", bufs=BANKS))
 
         def put(shape, dtype, name, at):
             return placed.tile(shape, dtype, name=name, offset=at, align_bytes=64)
@@ -64,16 +86,19 @@ def tile_list_speech_noise_suppression_kernel(
         nc.sync.dma_start(pick[:], offs)
         place = keep.tile([P, S // PER_COL], U16, name="place")
         nc.sync.dma_start(place[:], offs2)
-        tab_w = [put([P, T], I32, "tab_w0", 0), put([P, T], I32, "tab_w1", 52 * KB)]
+        tab_w = [put([P, T], I32, "tab_w0", AT_TABLE[0]), put([P, T], I32, "tab_w1", AT_TABLE[1])]
         nc.sync.dma_start(out=tab_w[0][:], in_=tab_words[0].rearrange("p n i -> p (n i)").bitcast(I32))
-        raw = {(a, 0): put([P, PACK, H // 2], F32, f"raw_low{a}", (70 + 4 * a) * KB) for a in range(PASSES)}
+        raw = {(a, 0): put([P, PACK, H // 2], F32, f"raw_low{a}", AT_RAW_LOW[a]) for a in range(PASSES)}
         for a in range(PASSES):
             load_w1(raw[a, 0], a, 0)
         nc.sync.dma_start(out=tab_w[1][:], in_=tab_words[1].rearrange("p n i -> p (n i)").bitcast(I32))
 
         nc.gpsimd.memset(tab_s[QUAD : 2 * QUAD, :].bitcast(I32), 0)
         nc.gpsimd.memset(tab_s[2 * QUAD : P, :].bitcast(I32), 0)
-        v_s = [keep.tile([P, PASSES * BANK], U8, name="v_s0", align_bytes=64), put([P, PASSES * BANK], U8, "v_s1", 12 * KB)]
+        v_s = [
+            keep.tile([P, PASSES * BANK], U8, name="v_s0", align_bytes=64),
+            put([P, PASSES * BANK], U8, "v_s1", AT_LATE_SCALES),
+        ]
         nc.vector.memset(v_s[0][:].bitcast(I32), 0)
         warm = keep.tile([P, 2], F32, name="warm")
         nc.vector.memset(warm[:, 0:1], 1.0)
@@ -106,7 +131,7 @@ def tile_list_speech_noise_suppression_kernel(
             for a in range(PASSES)
             if (s, a) != (1, 1)
         }
-        w1_c[1, 1] = put([P, P], U32, "w1_c11", 93 * KB)
+        w1_c[1, 1] = put([P, P], U32, "w1_c11", AT_LATE_CODES)
         w1_s = [keep.tile([P, PASSES * P], U8, name=f"w1_s{s}", align_bytes=64) for s in range(PACK)]
         grouped = {}
 
@@ -142,7 +167,7 @@ def tile_list_speech_noise_suppression_kernel(
 
         for a in range(PASSES):
             for t0 in (0, 2):
-                cast(a, 0, t0, (78 + 8 * a + t0 // 2) * KB)
+                cast(a, 0, t0, AT_ROUNDED_LOW[a] + t0 // 2 * KB)
                 quantise(a, 0, t0)
 
         v_last = [keep.tile([P, BANK], U32, name=f"v_last{b}", align_bytes=64) for b in range(HALVES)]
@@ -155,18 +180,20 @@ def tile_list_speech_noise_suppression_kernel(
 
         wgs_rows = wgs.rearrange("(p t) j -> p t j", t=PACK)
 
-        def load_wgs(tile, rows, j0, w):
+        def load_wgs(tile, planes, j0, w):
             for q in QUARTERS:
-                nc.sync.dma_start(out=tile[QUAD * q : QUAD * (q + 1), :], in_=wgs_rows[:, rows[q // 2], j0 : j0 + w])
+                nc.sync.dma_start(
+                    out=tile[QUAD * q : QUAD * (q + 1), :], in_=wgs_rows[:, planes[q // 2], j0 : j0 + w]
+                )
 
-        wg_low = put([P, S], F32, "wg_low", 0)
+        wg_low = put([P, S], F32, "wg_low", AT_WGS_LOW)
         for a in range(PASSES):
-            raw[a, 1] = put([P, PACK, H // 2], F32, f"raw_high{a}", (4 + 4 * a) * KB)
+            raw[a, 1] = put([P, PACK, H // 2], F32, f"raw_high{a}", AT_RAW_HIGH[a])
             load_w1(raw[a, 1], a, 1)
-            load_wgs(wg_low[:, BANK * a : BANK * (a + 1)], (0, 1), BANK * a, BANK)
             if a == 0:
                 move_scales(1)
-        wg_high = {2: put([P, S], F32, "wg2", 13 * KB), 3: put([P, S], F32, "wg3", 52 * KB)}
+            load_wgs(wg_low[:, BANK * a : BANK * (a + 1)], (0, 1), BANK * a, BANK)
+        wg_high = {t: put([P, S], F32, f"wg{t}", AT_WGS_HIGH[t]) for t in (2, 3)}
         for t in (2, 3):
             load_wgs(wg_high[t][:], (t, t), 0, S)
         w4_w = keep.tile([P, 2 * N], U8, name="w4_w", tag="picked", align_bytes=64)
@@ -183,20 +210,20 @@ def tile_list_speech_noise_suppression_kernel(
             mine = range(len(base_sb), len(base_sb) + count)
             c0 = starts[mine[0]]
             width = sum(CHUNKS[i] for i in mine)
-            tile = put([P, PACK, width], F32, f"base{c0}", 56 * KB + 16 * c0)
+            tile = put([P, PACK, width], F32, f"base{c0}", AT_BASE + PACK * WORD * c0)
             nc.sync.dma_start(out=tile[:], in_=base_rows[:, :, c0 : c0 + width])
             base_sb.extend([tile[:, :, starts[i] - c0 : starts[i] - c0 + CHUNKS[i]] for i in mine])
 
         h = {s: keep.tile([P, S], F32, name=f"h{s}") for s in (0, 2, 3)}
-        h_late = put([P, BANK], F32, "h_late", 8 * KB)
-        first_abs = put([P, S], F32, "first_abs", 94 * KB)
-        h[1] = put([P, S], F32, "h1", 95 * KB)
-        h_second = put([P, 256], F32, "h_second", 92 * KB)
+        h_late = put([P, BANK], F32, "h_late", AT_LATE_LOGS)
+        first_abs = put([P, S], F32, "first_abs", AT_FIRST_ABS)
+        h[1] = put([P, S], F32, "h1", AT_SLICE1_LOGS)
+        h_second = put([P, PIECE], F32, "h_second", AT_SECOND_LOGS)
 
         def logs(s, j0, w):
-            return {(0, 256): h_second[:], (0, BANK): h_late[:]}.get((s, j0), h[s][:, j0 : j0 + w])
+            return {(0, PIECE): h_second[:], (0, BANK): h_late[:]}.get((s, j0), h[s][:, j0 : j0 + w])
 
-        last_abs = put([P, PACK * T2], F32, "last_abs", 20 * KB)
+        last_abs = put([P, PACK * T2], F32, "last_abs", AT_GAIN)
 
         def make_h(s, j0, w):
             b, c0 = divmod(j0, BANK)
@@ -213,9 +240,14 @@ def tile_list_speech_noise_suppression_kernel(
                     start=a == order[0],
                     stop=a == order[1],
                 )
-            size = first_abs[:, 0:w] if s == 0 else last_abs[:, 0:w] if (s, j0 + w) == (PACK - 1, S) else logs(s, j0, w)
-            nc.scalar.activation(out=size, in_=y[:, 0:w], func=ACT.Abs)
-            nc.scalar.activation(out=logs(s, j0, w), in_=size, func=ACT.Ln, bias=1.0)
+            if s == 0:
+                magnitude = first_abs[:, 0:w]
+            elif (s, j0 + w) == (PACK - 1, S):
+                magnitude = last_abs[:, 0:w]
+            else:
+                magnitude = logs(s, j0, w)
+            nc.scalar.activation(out=magnitude, in_=y[:, 0:w], func=ACT.Abs)
+            nc.scalar.activation(out=logs(s, j0, w), in_=magnitude, func=ACT.Ln, bias=1.0)
 
         def scatter(s, j0, w):
             nc.vector.tensor_tensor(
@@ -225,16 +257,16 @@ def tile_list_speech_noise_suppression_kernel(
                 op=MULT,
             )
 
-        cast(0, 1, 0, 88 * KB, copy=nc.vector.tensor_copy)
+        cast(0, 1, 0, AT_ROUNDED_HIGH[0], copy=nc.vector.tensor_copy)
         quantise(0, 1, 0)
-        for j0 in (0, 256):
-            make_h(0, j0, 256)
-            scatter(0, j0, 256)
-        cast_whole(1, 1, 89 * KB)
+        for j0 in (0, PIECE):
+            make_h(0, j0, PIECE)
+            scatter(0, j0, PIECE)
+        cast_whole(1, 1, AT_ROUNDED_HIGH[1])
         quantise(1, 1, 0)
         make_h(0, BANK, BANK)
         scatter(0, BANK, BANK)
-        cast(0, 1, 2, 94 * KB)
+        cast(0, 1, 2, AT_FIRST_ABS)
         for a in range(PASSES):
             quantise(a, 1, 2)
         for s in (1, 2, 3):
@@ -249,7 +281,7 @@ def tile_list_speech_noise_suppression_kernel(
             mine = range(len(gain), len(gain) + count)
             c0 = starts[mine[0]]
             width = sum(CHUNKS[i] for i in mine)
-            tile = put([P, PACK, width], F32, f"gain{c0}", 20 * KB + 16 * c0)
+            tile = put([P, PACK, width], F32, f"gain{c0}", AT_GAIN + PACK * WORD * c0)
             groups.append((tile, c0, width))
             gain.extend([tile[:, :, starts[i] - c0 : starts[i] - c0 + CHUNKS[i]] for i in mine])
 
@@ -287,10 +319,9 @@ def tile_list_speech_noise_suppression_kernel(
             z_c = ring.tile([P, w], U32, name="z_c", align_bytes=64)
             z_s = ring.tile([P, w], U8, name="z_s", align_bytes=64)
             nc.vector.quantize_mx(out=z_c[:].bitcast(FP8X4), scales=z_s[:], in_=z[:])
-            per_bank = 2
-            for g0 in range(0, N // P, per_bank):
+            for g0 in range(0, N // P, GROUPS_PER_BANK):
                 acc = psum.tile([P, BANK], F32, name="bank")
-                for g in range(g0, g0 + per_bank):
+                for g in range(g0, g0 + GROUPS_PER_BANK):
                     nc.tensor.matmul_mx(
                         out=acc[:, (g - g0) * w : (g - g0 + 1) * w],
                         lhsT=w4_w[:, 2 * g * P : 2 * (g + 1) * P].bitcast(FP4X4),
@@ -300,14 +331,14 @@ def tile_list_speech_noise_suppression_kernel(
                         start=True,
                         stop=True,
                     )
-                res = stage.tile([P, per_bank * w], F32, name="res")
+                res = stage.tile([P, GROUPS_PER_BANK * w], F32, name="res")
                 if i >= len(CHUNKS) - 2 and (g0 > 0) == (i < len(CHUNKS) - 1):
-                    nc.vector.tensor_copy(out=res[:], in_=acc[:, 0 : per_bank * w])
+                    nc.vector.tensor_copy(out=res[:], in_=acc[:, 0 : GROUPS_PER_BANK * w])
                 else:
-                    nc.scalar.copy(out=res[:], in_=acc[:, 0 : per_bank * w])
+                    nc.scalar.copy(out=res[:], in_=acc[:, 0 : GROUPS_PER_BANK * w])
                 nc.sync.dma_start(
-                    out=out_rows[:, g0 : g0 + per_bank, starts[i] : starts[i] + w],
-                    in_=res[:].rearrange("p (g c) -> p g c", g=per_bank),
+                    out=out_rows[:, g0 : g0 + GROUPS_PER_BANK, starts[i] : starts[i] + w],
+                    in_=res[:].rearrange("p (g c) -> p g c", g=GROUPS_PER_BANK),
                 )
             if i + AHEAD < len(CHUNKS):
                 last_gain(i + AHEAD)

@@ -27,12 +27,13 @@ HALVES = S // BANK
 PER_COL = 16
 PAGES = 3
 PIECE = 256
-CHUNKS = (128,) + (256,) * 7 + (128,)
-BASE_LOADS = (2, 2, 2, 2, 1)
-GAIN_GROUPS = (1, 2, 2, 2, 2)
+WIDE = 256
+SOLO = 512
+GROUPS = (1, 2, 3)
+CHUNKS = ((0, 128),) + tuple((c0, WIDE) for c0 in range(SOLO, T2, WIDE)) + ((256, 256), (128, 128))
+FUSED = 640
 QUARTERS = (0, 2, 1, 3)
 AHEAD = 3
-FILL = 64
 GROUPS_PER_BANK = 2
 RING = 3
 STAGES = 16
@@ -46,6 +47,9 @@ AT_LATE_SCALES = 12 * KB
 AT_WGS_HIGH = {2: 13 * KB, 3: 52 * KB}
 AT_LATE_LOGS = AT_RAW_HIGH[1]
 AT_GAIN = 20 * KB
+AT_PARKED = (32 * KB, 103 * KB)
+AT_SOLO = 44 * KB
+AT_PARKED_SOLO = (99 * KB, 101 * KB)
 AT_BASE = 56 * KB
 AT_RAW_LOW = (70 * KB, 74 * KB)
 AT_ROUNDED_LOW = (78 * KB, 86 * KB)
@@ -204,15 +208,11 @@ def tile_list_speech_noise_suppression_kernel(
                 in_=w4_scales[0, 4 * q : 4 * q + 4, :].bitcast(I32),
             )
         base_rows = base.rearrange("(p t) c -> p t c", t=PACK)
-        starts = [sum(CHUNKS[:i]) for i in range(len(CHUNKS))]
-        base_sb = []
-        for count in BASE_LOADS:
-            mine = range(len(base_sb), len(base_sb) + count)
-            c0 = starts[mine[0]]
-            width = sum(CHUNKS[i] for i in mine)
-            tile = put([P, PACK, width], F32, f"base{c0}", AT_BASE + PACK * WORD * c0)
-            nc.sync.dma_start(out=tile[:], in_=base_rows[:, :, c0 : c0 + width])
-            base_sb.extend([tile[:, :, starts[i] - c0 : starts[i] - c0 + CHUNKS[i]] for i in mine])
+        spans = [(SOLO + WIDE * sum(GROUPS[:g]), WIDE * count) for g, count in enumerate(GROUPS)]
+        base_sb = {}
+        for c0, w in spans + [(0, SOLO)]:
+            base_sb[c0] = put([P, PACK, w], F32, f"base{c0}", AT_BASE + PACK * WORD * c0)
+            nc.sync.dma_start(out=base_sb[c0][:], in_=base_rows[:, :, c0 : c0 + w])
 
         h = {s: keep.tile([P, S], F32, name=f"h{s}") for s in (0, 2, 3)}
         h_late = put([P, BANK], F32, "h_late", AT_LATE_LOGS)
@@ -223,7 +223,20 @@ def tile_list_speech_noise_suppression_kernel(
         def logs(s, j0, w):
             return {(0, PIECE): h_second[:], (0, BANK): h_late[:]}.get((s, j0), h[s][:, j0 : j0 + w])
 
-        last_abs = put([P, PACK * T2], F32, "last_abs", AT_GAIN)
+        last_abs = put([P, 2 * (T2 - SOLO)], F32, "last_abs", AT_GAIN)
+        parked_pairs = [
+            put([P, 2 * (T2 - SOLO) + PACK * SOLO], F32, "parked0", AT_PARKED[0]),
+            put([P, T2 - SOLO], F32, "parked1", AT_PARKED[1]),
+        ]
+        parked_solo = [put([P, SOLO], F32, f"parked_solo{t}", AT_PARKED_SOLO[t]) for t in range(2)]
+
+        parked_first = put([P, WIDE * GROUPS[0]], F32, "parked_first", AT_GAIN + 2 * WORD * (spans[-1][0] - SOLO))
+
+        def parked(t, c0, w):
+            if (t, c0) == (0, SOLO):
+                return parked_first[:]
+            return parked_solo[t][:] if c0 < SOLO else parked_pairs[t][:, c0 - SOLO : c0 - SOLO + w]
+
 
         def make_h(s, j0, w):
             b, c0 = divmod(j0, BANK)
@@ -266,55 +279,99 @@ def tile_list_speech_noise_suppression_kernel(
         quantise(1, 1, 0)
         make_h(0, BANK, BANK)
         scatter(0, BANK, BANK)
+        second = spans[1][0]
+        for t, c0, w in ((1, SOLO, T2 - SOLO), (0, second, T2 - second), (1, 0, SOLO), (0, 0, SOLO)):
+            nc.sync.dma_start(out=parked(t, c0, w)[0:MID, :], in_=pages[0][MID * t : MID * (t + 1), c0 : c0 + w])
         cast(0, 1, 2, AT_FIRST_ABS)
         for a in range(PASSES):
             quantise(a, 1, 2)
         for s in (1, 2, 3):
             for j0 in (0, BANK):
                 make_h(s, j0, BANK)
-        for s in (1, 2):
-            scatter(s, 0, S)
 
-        groups = []
-        gain = []
-        for count in GAIN_GROUPS:
-            mine = range(len(gain), len(gain) + count)
-            c0 = starts[mine[0]]
-            width = sum(CHUNKS[i] for i in mine)
-            tile = put([P, PACK, width], F32, f"gain{c0}", AT_GAIN + PACK * WORD * c0)
-            groups.append((tile, c0, width))
-            gain.extend([tile[:, :, starts[i] - c0 : starts[i] - c0 + CHUNKS[i]] for i in mine])
+        def weigh(engine, s, j0):
+            tile = keep.tile([P, S - j0], F32, name=f"weighted{s}")
+            engine.tensor_tensor(
+                out=tile[:], in0=h[s][:, j0:S], in1=(wg_low if s < 2 else wg_high[s])[:, j0:S], op=MULT
+            )
+            return tile
+
+        def scatter_copy(s, j0, tile):
+            nc.vector.tensor_copy(out=pages[s % PAGES][:].indirect(place[:, j0 // PER_COL :]), in_=tile[:])
+
+        rest = weigh(nc.vector, 1, FUSED)
+        scatter(1, 0, FUSED)
+        scatter_copy(1, FUSED, rest)
+        weighted = {s: weigh(nc.gpsimd, s, 0) for s in (2, 3)}
+        scatter_copy(2, 0, weighted[2])
 
         def make_gain(dst, src):
             nc.scalar.activation(out=dst, in_=src, func=ACT.Exp, scale=-1.0)
 
-        for tile, c0, w in groups:
-            make_gain(tile[:, 0, :], pages[0][:, c0 : c0 + w])
-            nc.sync.dma_start(out=tile[0:MID, 1, :], in_=tile[MID:P, 0, :])
-        scatter(3, 0, S)
-        for tile, c0, w in groups:
-            make_gain(tile[0:MID, 3, :], pages[1][0:MID, c0 : c0 + w])
-            nc.sync.dma_start(out=tile[MID:P, 0, :], in_=tile[0:MID, 3, :])
-        for tile, c0, w in groups:
-            make_gain(tile[MID:P, 1, :], pages[1][MID:P, c0 : c0 + w])
-        for tile, c0, w in groups:
-            make_gain(tile[:, 2, :], pages[2][:, c0 : c0 + w])
+        nc.sync.dma_start(out=parked_first[0:MID, :], in_=pages[0][0:MID, SOLO:second])
+        for c0, w in spans + [(0, SOLO)]:
+            nc.sync.dma_start(out=parked(0, c0, w)[MID:P, :], in_=pages[1][0:MID, c0 : c0 + w])
+
+        def plane1(dst, c0, w):
+            make_gain(dst[0:MID, :], parked(1, c0, w)[0:MID, :])
+            make_gain(dst[MID:P, :], pages[1][MID:P, c0 : c0 + w])
+
+        low = [put([P, 2, w], F32, f"low{c0}", AT_GAIN + 2 * WORD * (c0 - SOLO)) for c0, w in spans]
+        pairs = {}
+        plane1(low[0][:, 1, :], *spans[0])
+        for g, (c0, w) in enumerate(spans):
+            if g == 0:
+                plane1(low[1][:, 1, :], *spans[1])
+            elif g > 1:
+                plane1(low[g][:, 1, :], c0, w)
+            make_gain(low[g][:, 0, :], parked(0, c0, w))
+            both = keep.tile([P, w // WIDE, 2, 2 * WIDE], BF16, name=f"pairs{c0}")
+            nc.gpsimd.tensor_tensor(
+                out=both[:, :, 0, :].rearrange("p k (c t) -> p k c t", t=2),
+                in0=low[g][:].rearrange("p t (k c) -> p k c t", c=WIDE),
+                in1=base_sb[c0][:, 0:2, :].rearrange("p t (k c) -> p k c t", c=WIDE),
+                op=MULT,
+            )
+            for k in range(w // WIDE):
+                pairs[c0 + k * WIDE] = both[:, k, :, :]
+        scatter_copy(3, 0, weighted[3])
+        solo = put([P, PACK, SOLO], F32, "solo", AT_SOLO)
+        plane1(solo[:, 1, :], 0, SOLO)
+        make_gain(solo[:, 0, :], parked(0, 0, SOLO))
+        make_gain(solo[:, 2, :], pages[2][:, 0:SOLO])
+        high = {}
+        for c0, w in spans:
+            high[c0] = put([P, 2, w], F32, f"high{c0}", AT_PARKED[0] + 2 * WORD * (c0 - SOLO))
+            make_gain(high[c0][:, 0, :], pages[2][:, c0 : c0 + w])
+
+        def upper(c0, w):
+            if c0 < SOLO:
+                return solo[:, :, c0 : c0 + w], base_sb[0][:, :, c0 : c0 + w]
+            g0 = max(start for start in high if start <= c0)
+            return high[g0][:, :, c0 - g0 : c0 - g0 + w], base_sb[g0][:, 2:PACK, c0 - g0 : c0 - g0 + w]
 
         def last_gain(i):
-            make_gain(gain[i][:, PACK - 1, :], pages[0][:, starts[i] : starts[i] + CHUNKS[i]])
+            c0, w = CHUNKS[i]
+            make_gain(upper(c0, w)[0][:, 1 if c0 in pairs else PACK - 1, :], pages[0][:, c0 : c0 + w])
 
         for i in range(AHEAD):
             last_gain(i)
 
         out_rows = out.rearrange("(g p) c -> p g c", p=P)
-        for i, w in enumerate(CHUNKS):
+        for i, (c0, w) in enumerate(CHUNKS):
             z = ring.tile([P, PACK * w], BF16, name="z", align_bytes=64)
-            for c0, c1 in ((0, w),) if i == 0 else ((0, FILL), (FILL, w)):
-                nc.vector.tensor_tensor(
-                    out=z[:, PACK * c0 : PACK * c1].rearrange("p (c e t) -> p c t e", e=2, t=PACK),
-                    in0=gain[i][:, :, c0:c1].rearrange("p t (c e) -> p c t e", e=2),
-                    in1=base_sb[i][:, :, c0:c1].rearrange("p t (c e) -> p c t e", e=2),
-                    op=MULT,
+            gain, rows = upper(c0, w)
+            planes = 2 if c0 in pairs else PACK
+            nc.vector.tensor_tensor(
+                out=(pairs[c0][:, 1, :] if c0 in pairs else z[:]).rearrange("p (c e t) -> p c t e", e=2, t=planes),
+                in0=gain.rearrange("p t (c e) -> p c t e", e=2),
+                in1=rows.rearrange("p t (c e) -> p c t e", e=2),
+                op=MULT,
+            )
+            if c0 in pairs:
+                nc.vector.tensor_copy(
+                    out=z[:].bitcast(I32).rearrange("p (c u) -> p c u", u=2),
+                    in_=pairs[c0].bitcast(I32).rearrange("p u c -> p c u"),
                 )
             z_c = ring.tile([P, w], U32, name="z_c", align_bytes=64)
             z_s = ring.tile([P, w], U8, name="z_s", align_bytes=64)
@@ -337,7 +394,7 @@ def tile_list_speech_noise_suppression_kernel(
                 else:
                     nc.scalar.copy(out=res[:], in_=acc[:, 0 : GROUPS_PER_BANK * w])
                 nc.sync.dma_start(
-                    out=out_rows[:, g0 : g0 + GROUPS_PER_BANK, starts[i] : starts[i] + w],
+                    out=out_rows[:, g0 : g0 + GROUPS_PER_BANK, c0 : c0 + w],
                     in_=res[:].rearrange("p (g c) -> p g c", g=GROUPS_PER_BANK),
                 )
             if i + AHEAD < len(CHUNKS):

@@ -325,15 +325,14 @@ def tile_list_speech_noise_suppression_kernel(
             elif g > 1:
                 plane1(low[g][:, 1, :], c0, w)
             make_gain(low[g][:, 0, :], parked(0, c0, w))
-            both = keep.tile([P, w // WIDE, 2, 2 * WIDE], BF16, name=f"pairs{c0}")
-            nc.gpsimd.tensor_tensor(
-                out=both[:, :, 0, :].rearrange("p k (c t) -> p k c t", t=2),
-                in0=low[g][:].rearrange("p t (k c) -> p k c t", c=WIDE),
-                in1=base_sb[c0][:, 0:2, :].rearrange("p t (k c) -> p k c t", c=WIDE),
-                op=MULT,
-            )
-            for k in range(w // WIDE):
-                pairs[c0 + k * WIDE] = both[:, k, :, :]
+            for k0 in range(0, w, WIDE):
+                pairs[c0 + k0] = keep.tile([P, 2, 2 * WIDE], BF16, name=f"pairs{c0 + k0}")[:]
+                nc.gpsimd.tensor_tensor(
+                    out=pairs[c0 + k0][:, 0, :].rearrange("p (c e t) -> p c t e", e=4, t=2),
+                    in0=low[g][:, :, k0 : k0 + WIDE].rearrange("p t (c e) -> p c t e", e=4),
+                    in1=base_sb[c0][:, 0:2, k0 : k0 + WIDE].rearrange("p t (c e) -> p c t e", e=4),
+                    op=MULT,
+                )
         scatter_copy(3, 0, weighted[3])
         solo = put([P, PACK, SOLO], F32, "solo", AT_SOLO)
         plane1(solo[:, 1, :], 0, SOLO)

@@ -50,6 +50,7 @@ AT_GAIN = 20 * KB
 AT_PARKED = (32 * KB, 103 * KB)
 AT_SOLO = 44 * KB
 AT_PARKED_SOLO = (99 * KB, 101 * KB)
+AT_BASE_LOW = 76 * KB
 AT_BASE = 56 * KB
 AT_RAW_LOW = (70 * KB, 74 * KB)
 AT_ROUNDED_LOW = (78 * KB, 86 * KB)
@@ -209,10 +210,10 @@ def tile_list_speech_noise_suppression_kernel(
             )
         base_rows = base.rearrange("(p t) c -> p t c", t=PACK)
         spans = [(SOLO + WIDE * sum(GROUPS[:g]), WIDE * count) for g, count in enumerate(GROUPS)]
-        base_sb = {}
-        for c0, w in spans + [(0, SOLO)]:
-            base_sb[c0] = put([P, PACK, w], F32, f"base{c0}", AT_BASE + PACK * WORD * c0)
-            nc.sync.dma_start(out=base_sb[c0][:], in_=base_rows[:, :, c0 : c0 + w])
+        base_low = {}
+        for c0, w in spans:
+            base_low[c0] = put([P, 2, w], F32, f"base_low{c0}", AT_BASE_LOW + 2 * WORD * (c0 - SOLO))
+            nc.sync.dma_start(out=base_low[c0][:], in_=base_rows[:, 0:2, c0 : c0 + w])
 
         h = {s: keep.tile([P, S], F32, name=f"h{s}") for s in (0, 2, 3)}
         h_late = put([P, BANK], F32, "h_late", AT_LATE_LOGS)
@@ -223,7 +224,7 @@ def tile_list_speech_noise_suppression_kernel(
         def logs(s, j0, w):
             return {(0, PIECE): h_second[:], (0, BANK): h_late[:]}.get((s, j0), h[s][:, j0 : j0 + w])
 
-        last_abs = put([P, 2 * (T2 - SOLO)], F32, "last_abs", AT_GAIN)
+        last_abs = put([P, 2 * (spans[-1][0] - SOLO)], F32, "last_abs", AT_GAIN)
         parked_pairs = [
             put([P, 2 * (T2 - SOLO) + PACK * SOLO], F32, "parked0", AT_PARKED[0]),
             put([P, T2 - SOLO], F32, "parked1", AT_PARKED[1]),
@@ -280,7 +281,8 @@ def tile_list_speech_noise_suppression_kernel(
         make_h(0, BANK, BANK)
         scatter(0, BANK, BANK)
         second = spans[1][0]
-        for t, c0, w in ((1, SOLO, T2 - SOLO), (0, second, T2 - second), (1, 0, SOLO), (0, 0, SOLO)):
+        early = ((1, SOLO, T2 - SOLO), (0, SOLO, second - SOLO), (0, second, T2 - second), (1, 0, SOLO), (0, 0, SOLO))
+        for t, c0, w in early:
             nc.sync.dma_start(out=parked(t, c0, w)[0:MID, :], in_=pages[0][MID * t : MID * (t + 1), c0 : c0 + w])
         cast(0, 1, 2, AT_FIRST_ABS)
         for a in range(PASSES):
@@ -290,14 +292,17 @@ def tile_list_speech_noise_suppression_kernel(
                 make_h(s, j0, BANK)
 
         def weigh(engine, s, j0):
-            tile = keep.tile([P, S - j0], F32, name=f"weighted{s}")
+            if s == 1:
+                tile = put([P, (AT_BASE_LOW - AT_BASE) // WORD], F32, "weighted1", AT_BASE)[:, 0 : S - j0]
+            else:
+                tile = keep.tile([P, S - j0], F32, name=f"weighted{s}")[:]
             engine.tensor_tensor(
-                out=tile[:], in0=h[s][:, j0:S], in1=(wg_low if s < 2 else wg_high[s])[:, j0:S], op=MULT
+                out=tile, in0=h[s][:, j0:S], in1=(wg_low if s < 2 else wg_high[s])[:, j0:S], op=MULT
             )
             return tile
 
         def scatter_copy(s, j0, tile):
-            nc.vector.tensor_copy(out=pages[s % PAGES][:].indirect(place[:, j0 // PER_COL :]), in_=tile[:])
+            nc.vector.tensor_copy(out=pages[s % PAGES][:].indirect(place[:, j0 // PER_COL :]), in_=tile)
 
         rest = weigh(nc.vector, 1, FUSED)
         scatter(1, 0, FUSED)
@@ -308,9 +313,15 @@ def tile_list_speech_noise_suppression_kernel(
         def make_gain(dst, src):
             nc.scalar.activation(out=dst, in_=src, func=ACT.Exp, scale=-1.0)
 
-        nc.sync.dma_start(out=parked_first[0:MID, :], in_=pages[0][0:MID, SOLO:second])
         for c0, w in spans + [(0, SOLO)]:
             nc.sync.dma_start(out=parked(0, c0, w)[MID:P, :], in_=pages[1][0:MID, c0 : c0 + w])
+
+        base_solo = put([P, PACK, SOLO], F32, "base_solo", AT_BASE)
+        nc.sync.dma_start(out=base_solo[:], in_=base_rows[:, :, 0:SOLO])
+        base_high = {}
+        for c0, w in spans:
+            base_high[c0] = put([P, 2, w], F32, f"base_high{c0}", AT_BASE + WORD * (PACK * SOLO + 2 * (c0 - SOLO)))
+            nc.sync.dma_start(out=base_high[c0][:], in_=base_rows[:, 2:PACK, c0 : c0 + w])
 
         def plane1(dst, c0, w):
             make_gain(dst[0:MID, :], parked(1, c0, w)[0:MID, :])
@@ -330,7 +341,7 @@ def tile_list_speech_noise_suppression_kernel(
                 nc.gpsimd.tensor_tensor(
                     out=pairs[c0 + k0][:, 0, :].rearrange("p (c e t) -> p c t e", e=4, t=2),
                     in0=low[g][:, :, k0 : k0 + WIDE].rearrange("p t (c e) -> p c t e", e=4),
-                    in1=base_sb[c0][:, 0:2, k0 : k0 + WIDE].rearrange("p t (c e) -> p c t e", e=4),
+                    in1=base_low[c0][:, :, k0 : k0 + WIDE].rearrange("p t (c e) -> p c t e", e=4),
                     op=MULT,
                 )
         scatter_copy(3, 0, weighted[3])
@@ -345,9 +356,9 @@ def tile_list_speech_noise_suppression_kernel(
 
         def upper(c0, w):
             if c0 < SOLO:
-                return solo[:, :, c0 : c0 + w], base_sb[0][:, :, c0 : c0 + w]
+                return solo[:, :, c0 : c0 + w], base_solo[:, :, c0 : c0 + w]
             g0 = max(start for start in high if start <= c0)
-            return high[g0][:, :, c0 - g0 : c0 - g0 + w], base_sb[g0][:, 2:PACK, c0 - g0 : c0 - g0 + w]
+            return high[g0][:, :, c0 - g0 : c0 - g0 + w], base_high[g0][:, :, c0 - g0 : c0 - g0 + w]
 
         def last_gain(i):
             c0, w = CHUNKS[i]

@@ -28,9 +28,10 @@ PER_COL = 16
 PAGES = 3
 PIECE = 256
 WIDE = 256
-SOLO = 512
-GROUPS = (1, 2, 3)
-CHUNKS = ((0, 128),) + tuple((c0, WIDE) for c0 in range(SOLO, T2, WIDE)) + ((256, 256), (128, 128))
+GROUPS = (1, 2, 2)
+SOLO = T2 - WIDE * sum(GROUPS)
+WIDE_STARTS = tuple(range(SOLO, T2, WIDE)) + tuple(range(WIDE, SOLO, WIDE))
+CHUNKS = ((0, WIDE // 2),) + tuple((c0, WIDE) for c0 in WIDE_STARTS) + ((WIDE // 2, WIDE // 2),)
 FUSED = 640
 QUARTERS = (0, 2, 1, 3)
 AHEAD = 3
@@ -47,13 +48,14 @@ AT_LATE_SCALES = 12 * KB
 AT_WGS_HIGH = {2: 13 * KB, 3: 52 * KB}
 AT_LATE_LOGS = AT_RAW_HIGH[1]
 AT_GAIN = 20 * KB
-AT_PARKED = (32 * KB, 103 * KB)
-AT_SOLO = 44 * KB
-AT_PARKED_SOLO = (99 * KB, 101 * KB)
-AT_BASE_LOW = 76 * KB
+AT_PARKED = (AT_GAIN + 2 * WORD * (T2 - SOLO), 99 * KB + 2 * WORD * SOLO)
+AT_SOLO = AT_GAIN + 4 * WORD * (T2 - SOLO)
+AT_PARKED_SOLO = (99 * KB, 99 * KB + WORD * SOLO)
+AT_BASE_LOW = 82 * KB
+AT_LAST_LOW = AT_BASE_LOW - 2 * WORD * WIDE * GROUPS[-1]
 AT_BASE = 56 * KB
 AT_RAW_LOW = (70 * KB, 74 * KB)
-AT_ROUNDED_LOW = (78 * KB, 86 * KB)
+AT_ROUNDED_LOW = (82 * KB, 86 * KB)
 AT_ROUNDED_HIGH = (88 * KB, 89 * KB)
 AT_SECOND_LOGS = 92 * KB
 AT_LATE_CODES = 93 * KB
@@ -211,9 +213,13 @@ def tile_list_speech_noise_suppression_kernel(
         base_rows = base.rearrange("(p t) c -> p t c", t=PACK)
         spans = [(SOLO + WIDE * sum(GROUPS[:g]), WIDE * count) for g, count in enumerate(GROUPS)]
         base_low = {}
-        for c0, w in spans:
-            base_low[c0] = put([P, 2, w], F32, f"base_low{c0}", AT_BASE_LOW + 2 * WORD * (c0 - SOLO))
+
+        def load_low(c0, w, at):
+            base_low[c0] = put([P, 2, w], F32, f"base_low{c0}", at)
             nc.sync.dma_start(out=base_low[c0][:], in_=base_rows[:, 0:2, c0 : c0 + w])
+
+        for c0, w in spans[:-1]:
+            load_low(c0, w, AT_BASE_LOW + 2 * WORD * (c0 - SOLO))
 
         h = {s: keep.tile([P, S], F32, name=f"h{s}") for s in (0, 2, 3)}
         h_late = put([P, BANK], F32, "h_late", AT_LATE_LOGS)
@@ -314,6 +320,8 @@ def tile_list_speech_noise_suppression_kernel(
             nc.scalar.activation(out=dst, in_=src, func=ACT.Exp, scale=-1.0)
 
         for c0, w in spans + [(0, SOLO)]:
+            if c0 < SOLO:
+                load_low(*spans[-1], AT_LAST_LOW)
             nc.sync.dma_start(out=parked(0, c0, w)[MID:P, :], in_=pages[1][0:MID, c0 : c0 + w])
 
         base_solo = put([P, PACK, SOLO], F32, "base_solo", AT_BASE)

@@ -28,16 +28,16 @@ PER_COL = 16
 PAGES = 3
 PIECE = 256
 WIDE = 256
-GROUPS = (1, 2, 2)
+GROUPS = (1, 2, 3)
 SOLO = T2 - WIDE * sum(GROUPS)
-WIDE_STARTS = tuple(range(SOLO, T2, WIDE)) + tuple(range(WIDE, SOLO, WIDE))
-CHUNKS = ((0, WIDE // 2),) + tuple((c0, WIDE) for c0 in WIDE_STARTS) + ((WIDE // 2, WIDE // 2),)
+CHUNKS = ((0, WIDE // 2), (WIDE // 2, WIDE // 2)) + tuple((c0, WIDE) for c0 in range(WIDE, T2, WIDE))
+JOINED = T2 // 2
 FUSED = 640
 QUARTERS = (0, 2, 1, 3)
 AHEAD = 3
 GROUPS_PER_BANK = 2
 RING = 3
-STAGES = 16
+STAGES = 10
 
 KB = 1024
 WORD = 4
@@ -376,6 +376,7 @@ def tile_list_speech_noise_suppression_kernel(
             last_gain(i)
 
         out_rows = out.rearrange("(g p) c -> p g c", p=P)
+        joined = {}
         for i, (c0, w) in enumerate(CHUNKS):
             z = ring.tile([P, PACK * w], BF16, name="z", align_bytes=64)
             gain, rows = upper(c0, w)
@@ -406,14 +407,23 @@ def tile_list_speech_noise_suppression_kernel(
                         start=True,
                         stop=True,
                     )
-                res = stage.tile([P, GROUPS_PER_BANK * w], F32, name="res")
-                if i >= len(CHUNKS) - 2 and (g0 > 0) == (i < len(CHUNKS) - 1):
-                    nc.vector.tensor_copy(out=res[:], in_=acc[:, 0 : GROUPS_PER_BANK * w])
+                if c0 < JOINED:
+                    first_frame, width = c0, w
+                    res = stage.tile([P, GROUPS_PER_BANK, w], F32, name="res")
                 else:
-                    nc.scalar.copy(out=res[:], in_=acc[:, 0 : GROUPS_PER_BANK * w])
-                nc.sync.dma_start(
-                    out=out_rows[:, g0 : g0 + GROUPS_PER_BANK, c0 : c0 + w],
-                    in_=res[:].rearrange("p (g c) -> p g c", g=GROUPS_PER_BANK),
-                )
+                    first_frame, width = c0 - c0 % (2 * w), 2 * w
+                    if c0 == first_frame:
+                        joined[g0] = keep.tile([P, GROUPS_PER_BANK, width], F32, name=f"joined{c0}_{g0}")
+                    res = joined[g0]
+                dst = res[:, :, c0 - first_frame : c0 - first_frame + w]
+                src = acc[:, 0 : GROUPS_PER_BANK * w].rearrange("p (g c) -> p g c", g=GROUPS_PER_BANK)
+                if i == len(CHUNKS) - 1 and g0 == 0:
+                    nc.vector.tensor_copy(out=dst, in_=src)
+                else:
+                    nc.scalar.copy(out=dst, in_=src)
+                if c0 + w == first_frame + width:
+                    nc.sync.dma_start(
+                        out=out_rows[:, g0 : g0 + GROUPS_PER_BANK, first_frame : first_frame + width], in_=res[:]
+                    )
             if i + AHEAD < len(CHUNKS):
                 last_gain(i + AHEAD)

@@ -28,10 +28,11 @@ PER_COL = 16
 PAGES = 3
 PIECE = 256
 WIDE = 256
-GROUPS = (1, 2, 3)
+GROUPS = (1, 1, 2, 3)
 SOLO = T2 - WIDE * sum(GROUPS)
 CHUNKS = ((0, WIDE // 2), (WIDE // 2, WIDE // 2)) + tuple((c0, WIDE) for c0 in range(WIDE, T2, WIDE))
 JOINED = T2 // 2
+FILL = 64
 FUSED = 640
 QUARTERS = (0, 2, 1, 3)
 AHEAD = 3
@@ -51,11 +52,12 @@ AT_GAIN = 20 * KB
 AT_PARKED = (AT_GAIN + 2 * WORD * (T2 - SOLO), 99 * KB + 2 * WORD * SOLO)
 AT_SOLO = AT_GAIN + 4 * WORD * (T2 - SOLO)
 AT_PARKED_SOLO = (99 * KB, 99 * KB + WORD * SOLO)
-AT_BASE_LOW = 82 * KB
-AT_LAST_LOW = AT_BASE_LOW - 2 * WORD * WIDE * GROUPS[-1]
+EARLY = 2
+AT_BASE_LOW = 84 * KB
+AT_LATE_LOW = AT_BASE_LOW - 2 * WORD * (T2 - SOLO)
 AT_BASE = 56 * KB
 AT_RAW_LOW = (70 * KB, 74 * KB)
-AT_ROUNDED_LOW = (82 * KB, 86 * KB)
+AT_ROUNDED_LOW = (84 * KB, 86 * KB)
 AT_ROUNDED_HIGH = (88 * KB, 89 * KB)
 AT_SECOND_LOGS = 92 * KB
 AT_LATE_CODES = 93 * KB
@@ -218,7 +220,7 @@ def tile_list_speech_noise_suppression_kernel(
             base_low[c0] = put([P, 2, w], F32, f"base_low{c0}", at)
             nc.sync.dma_start(out=base_low[c0][:], in_=base_rows[:, 0:2, c0 : c0 + w])
 
-        for c0, w in spans[:-1]:
+        for c0, w in spans[:EARLY]:
             load_low(c0, w, AT_BASE_LOW + 2 * WORD * (c0 - SOLO))
 
         h = {s: keep.tile([P, S], F32, name=f"h{s}") for s in (0, 2, 3)}
@@ -230,18 +232,19 @@ def tile_list_speech_noise_suppression_kernel(
         def logs(s, j0, w):
             return {(0, PIECE): h_second[:], (0, BANK): h_late[:]}.get((s, j0), h[s][:, j0 : j0 + w])
 
-        last_abs = put([P, 2 * (spans[-1][0] - SOLO)], F32, "last_abs", AT_GAIN)
+        last_abs = put([P, 2 * (spans[EARLY][0] - SOLO)], F32, "last_abs", AT_GAIN)
         parked_pairs = [
             put([P, 2 * (T2 - SOLO) + PACK * SOLO], F32, "parked0", AT_PARKED[0]),
             put([P, T2 - SOLO], F32, "parked1", AT_PARKED[1]),
         ]
         parked_solo = [put([P, SOLO], F32, f"parked_solo{t}", AT_PARKED_SOLO[t]) for t in range(2)]
 
-        parked_first = put([P, WIDE * GROUPS[0]], F32, "parked_first", AT_GAIN + 2 * WORD * (spans[-1][0] - SOLO))
+        later = spans[EARLY][0]
+        parked_first = put([P, 2 * (T2 - later)], F32, "parked_first", AT_GAIN + 2 * WORD * (later - SOLO))
 
         def parked(t, c0, w):
             if (t, c0) == (0, SOLO):
-                return parked_first[:]
+                return parked_first[:, 0:w]
             return parked_solo[t][:] if c0 < SOLO else parked_pairs[t][:, c0 - SOLO : c0 - SOLO + w]
 
 
@@ -297,31 +300,33 @@ def tile_list_speech_noise_suppression_kernel(
             for j0 in (0, BANK):
                 make_h(s, j0, BANK)
 
-        def weigh(engine, s, j0):
+        def weigh(engine, s, j0, w):
             if s == 1:
-                tile = put([P, (AT_BASE_LOW - AT_BASE) // WORD], F32, "weighted1", AT_BASE)[:, 0 : S - j0]
+                tile = put([P, (AT_BASE_LOW - AT_BASE) // WORD], F32, "weighted1", AT_BASE)[:, 0:w]
             else:
-                tile = keep.tile([P, S - j0], F32, name=f"weighted{s}")[:]
+                tile = keep.tile([P, w], F32, name=f"weighted{s}_{j0}")[:]
             engine.tensor_tensor(
-                out=tile, in0=h[s][:, j0:S], in1=(wg_low if s < 2 else wg_high[s])[:, j0:S], op=MULT
+                out=tile, in0=h[s][:, j0 : j0 + w], in1=(wg_low if s < 2 else wg_high[s])[:, j0 : j0 + w], op=MULT
             )
             return tile
 
-        def scatter_copy(s, j0, tile):
-            nc.vector.tensor_copy(out=pages[s % PAGES][:].indirect(place[:, j0 // PER_COL :]), in_=tile)
+        def scatter_copy(s, j0, w, tile):
+            nc.vector.tensor_copy(
+                out=pages[s % PAGES][:].indirect(place[:, j0 // PER_COL : (j0 + w) // PER_COL]), in_=tile
+            )
 
-        rest = weigh(nc.vector, 1, FUSED)
         scatter(1, 0, FUSED)
-        scatter_copy(1, FUSED, rest)
-        weighted = {s: weigh(nc.gpsimd, s, 0) for s in (2, 3)}
-        scatter_copy(2, 0, weighted[2])
+        scatter_copy(1, FUSED, S - FUSED, weigh(nc.vector, 1, FUSED, S - FUSED))
+        for s in (2, 3):
+            scatter_copy(s, 0, S, weigh(nc.gpsimd, s, 0, S))
 
         def make_gain(dst, src):
             nc.scalar.activation(out=dst, in_=src, func=ACT.Exp, scale=-1.0)
 
         for c0, w in spans + [(0, SOLO)]:
             if c0 < SOLO:
-                load_low(*spans[-1], AT_LAST_LOW)
+                for late, width in spans[EARLY:]:
+                    load_low(late, width, AT_LATE_LOW + 2 * WORD * (late - SOLO))
             nc.sync.dma_start(out=parked(0, c0, w)[MID:P, :], in_=pages[1][0:MID, c0 : c0 + w])
 
         base_solo = put([P, PACK, SOLO], F32, "base_solo", AT_BASE)
@@ -344,15 +349,15 @@ def tile_list_speech_noise_suppression_kernel(
             elif g > 1:
                 plane1(low[g][:, 1, :], c0, w)
             make_gain(low[g][:, 0, :], parked(0, c0, w))
+            both = keep.tile([P, 2, 2 * w], BF16, name=f"pairs{c0}")
+            nc.gpsimd.tensor_tensor(
+                out=both[:, 0, :].rearrange("p (c e t) -> p c t e", e=4, t=2),
+                in0=low[g][:].rearrange("p t (c e) -> p c t e", e=4),
+                in1=base_low[c0][:].rearrange("p t (c e) -> p c t e", e=4),
+                op=MULT,
+            )
             for k0 in range(0, w, WIDE):
-                pairs[c0 + k0] = keep.tile([P, 2, 2 * WIDE], BF16, name=f"pairs{c0 + k0}")[:]
-                nc.gpsimd.tensor_tensor(
-                    out=pairs[c0 + k0][:, 0, :].rearrange("p (c e t) -> p c t e", e=4, t=2),
-                    in0=low[g][:, :, k0 : k0 + WIDE].rearrange("p t (c e) -> p c t e", e=4),
-                    in1=base_low[c0][:, :, k0 : k0 + WIDE].rearrange("p t (c e) -> p c t e", e=4),
-                    op=MULT,
-                )
-        scatter_copy(3, 0, weighted[3])
+                pairs[c0 + k0] = both[:, :, 2 * k0 : 2 * (k0 + WIDE)]
         solo = put([P, PACK, SOLO], F32, "solo", AT_SOLO)
         plane1(solo[:, 1, :], 0, SOLO)
         make_gain(solo[:, 0, :], parked(0, 0, SOLO))
@@ -381,12 +386,14 @@ def tile_list_speech_noise_suppression_kernel(
             z = ring.tile([P, PACK * w], BF16, name="z", align_bytes=64)
             gain, rows = upper(c0, w)
             planes = 2 if c0 in pairs else PACK
-            nc.vector.tensor_tensor(
-                out=(pairs[c0][:, 1, :] if c0 in pairs else z[:]).rearrange("p (c e t) -> p c t e", e=2, t=planes),
-                in0=gain.rearrange("p t (c e) -> p c t e", e=2),
-                in1=rows.rearrange("p t (c e) -> p c t e", e=2),
-                op=MULT,
-            )
+            product = pairs[c0][:, 1, :] if c0 in pairs else z[:]
+            for f0, f1 in ((0, FILL), (FILL, w)) if i == 1 else ((0, w),):
+                nc.vector.tensor_tensor(
+                    out=product[:, planes * f0 : planes * f1].rearrange("p (c e t) -> p c t e", e=2, t=planes),
+                    in0=gain[:, :, f0:f1].rearrange("p t (c e) -> p c t e", e=2),
+                    in1=rows[:, :, f0:f1].rearrange("p t (c e) -> p c t e", e=2),
+                    op=MULT,
+                )
             if c0 in pairs:
                 nc.vector.tensor_copy(
                     out=z[:].bitcast(I32).rearrange("p (c u) -> p c u", u=2),

@@ -32,7 +32,7 @@ GROUPS = (1, 1, 2, 3)
 SOLO = T2 - WIDE * sum(GROUPS)
 CHUNKS = ((0, WIDE // 2), (WIDE // 2, WIDE // 2)) + tuple((c0, WIDE) for c0 in range(WIDE, T2, WIDE))
 JOINED = T2 // 2
-FILL = 64
+WOVEN_BY_SCALAR = 3
 FUSED = 640
 QUARTERS = (0, 2, 1, 3)
 AHEAD = 3
@@ -387,7 +387,7 @@ def tile_list_speech_noise_suppression_kernel(
             gain, rows = upper(c0, w)
             planes = 2 if c0 in pairs else PACK
             product = pairs[c0][:, 1, :] if c0 in pairs else z[:]
-            for f0, f1 in ((0, FILL), (FILL, w)) if i == 1 else ((0, w),):
+            for f0, f1 in ((0, w // 2), (w // 2, w)) if i in (1, WOVEN_BY_SCALAR) else ((0, w),):
                 nc.vector.tensor_tensor(
                     out=product[:, planes * f0 : planes * f1].rearrange("p (c e t) -> p c t e", e=2, t=planes),
                     in0=gain[:, :, f0:f1].rearrange("p t (c e) -> p c t e", e=2),
@@ -395,9 +395,11 @@ def tile_list_speech_noise_suppression_kernel(
                     op=MULT,
                 )
             if c0 in pairs:
-                nc.vector.tensor_copy(
-                    out=z[:].bitcast(I32).rearrange("p (c u) -> p c u", u=2),
-                    in_=pairs[c0].bitcast(I32).rearrange("p u c -> p c u"),
+                weave = nc.scalar.copy if i == WOVEN_BY_SCALAR else nc.vector.tensor_copy
+                words = U32 if i == WOVEN_BY_SCALAR else I32
+                weave(
+                    out=z[:].bitcast(words).rearrange("p (c u) -> p c u", u=2),
+                    in_=pairs[c0].bitcast(words).rearrange("p u c -> p c u"),
                 )
             z_c = ring.tile([P, w], U32, name="z_c", align_bytes=64)
             z_s = ring.tile([P, w], U8, name="z_s", align_bytes=64)

@@ -31,14 +31,14 @@ WIDE = 256
 GROUPS = (1, 1, 2, 3)
 SOLO = T2 - WIDE * sum(GROUPS)
 CHUNKS = ((0, WIDE // 2), (WIDE // 2, WIDE // 2)) + tuple((c0, WIDE) for c0 in range(WIDE, T2, WIDE))
-JOINED = T2 // 2
+JOINED = 2 * WIDE
 WOVEN_BY_SCALAR = 3
 FUSED = 640
 QUARTERS = (0, 2, 1, 3)
 AHEAD = 3
 GROUPS_PER_BANK = 2
 RING = 3
-STAGES = 10
+STAGES = 8
 
 KB = 1024
 WORD = 4
@@ -404,7 +404,9 @@ def tile_list_speech_noise_suppression_kernel(
             z_c = ring.tile([P, w], U32, name="z_c", align_bytes=64)
             z_s = ring.tile([P, w], U8, name="z_s", align_bytes=64)
             nc.vector.quantize_mx(out=z_c[:].bitcast(FP8X4), scales=z_s[:], in_=z[:])
-            for g0 in range(0, N // P, GROUPS_PER_BANK):
+            turn = c0 // WIDE % 2 if c0 >= JOINED else 1
+            for bank in (1 - turn, turn):
+                g0 = bank * GROUPS_PER_BANK
                 acc = psum.tile([P, BANK], F32, name="bank")
                 for g in range(g0, g0 + GROUPS_PER_BANK):
                     nc.tensor.matmul_mx(
@@ -416,17 +418,20 @@ def tile_list_speech_noise_suppression_kernel(
                         start=True,
                         stop=True,
                     )
-                if c0 < JOINED:
+                if bank in joined:
+                    first_frame, width = c0 - w, 2 * w
+                    res = joined[bank]
+                    joined = {}
+                elif c0 >= JOINED and c0 + w < T2 and bank == turn:
+                    first_frame, width = c0, 2 * w
+                    res = keep.tile([P, GROUPS_PER_BANK, width], F32, name=f"joined{c0}")
+                    joined = {bank: res}
+                else:
                     first_frame, width = c0, w
                     res = stage.tile([P, GROUPS_PER_BANK, w], F32, name="res")
-                else:
-                    first_frame, width = c0 - c0 % (2 * w), 2 * w
-                    if c0 == first_frame:
-                        joined[g0] = keep.tile([P, GROUPS_PER_BANK, width], F32, name=f"joined{c0}_{g0}")
-                    res = joined[g0]
                 dst = res[:, :, c0 - first_frame : c0 - first_frame + w]
                 src = acc[:, 0 : GROUPS_PER_BANK * w].rearrange("p (g c) -> p g c", g=GROUPS_PER_BANK)
-                if i == len(CHUNKS) - 1 and g0 == 0:
+                if i == len(CHUNKS) - 1 and bank != turn:
                     nc.vector.tensor_copy(out=dst, in_=src)
                 else:
                     nc.scalar.copy(out=dst, in_=src)

from contextlib import ExitStack

import concourse.mybir as mybir

K, T, S, T2, H, N = 1024, 4096, 1024, 2048, 512, 512
FLOPS = 2 * K * H * S + 2 * H * N * T2

F32 = mybir.dt.float32
BF16 = mybir.dt.bfloat16
I32 = mybir.dt.int32
U32 = mybir.dt.uint32
U16 = mybir.dt.uint16
U8 = mybir.dt.uint8
FP8X4 = mybir.dt.float8_e4m3fn_x4
FP4X4 = mybir.dt.float4_e2m1fn_x4
ACT = mybir.ActivationFunctionType
MULT = mybir.AluOpType.mult

P = 128
PACK = 4
QUAD = 32
MID = P // 2
PASSES = K // (P * PACK)
BANK = 512
BANKS = 8
HALVES = S // BANK
PER_COL = 16
PAGES = 3
PIECE = 256
WIDE = 256
GROUPS = (1, 1, 2, 3)
SOLO = T2 - WIDE * sum(GROUPS)
CHUNKS = ((0, WIDE // 2), (WIDE // 2, WIDE // 2)) + tuple((c0, WIDE) for c0 in range(WIDE, T2, WIDE))
JOINED = 2 * WIDE
WOVEN_BY_SCALAR = 3
FUSED = 640
QUARTERS = (0, 2, 1, 3)
AHEAD = 3
GROUPS_PER_BANK = 2
RING = 3
STAGES = 8

KB = 1024
WORD = 4
AT_TABLE = (0, 52 * KB)
AT_WGS_LOW = 0
AT_RAW_HIGH = (4 * KB, 8 * KB)
AT_LATE_SCALES = 12 * KB
AT_WGS_HIGH = {2: 13 * KB, 3: 52 * KB}
AT_LATE_LOGS = AT_RAW_HIGH[1]
AT_GAIN = 20 * KB
AT_PARKED = (AT_GAIN + 2 * WORD * (T2 - SOLO), 99 * KB + 2 * WORD * SOLO)
AT_SOLO = AT_GAIN + 4 * WORD * (T2 - SOLO)
AT_PARKED_SOLO = (99 * KB, 99 * KB + WORD * SOLO)
EARLY = 2
AT_BASE_LOW = 84 * KB
AT_LATE_LOW = AT_BASE_LOW - 2 * WORD * (T2 - SOLO)
AT_BASE = 56 * KB
AT_RAW_LOW = (70 * KB, 74 * KB)
AT_ROUNDED_LOW = (84 * KB, 86 * KB)
AT_ROUNDED_HIGH = (88 * KB, 89 * KB)
AT_SECOND_LOGS = 92 * KB
AT_LATE_CODES = 93 * KB
AT_FIRST_ABS = 94 * KB
AT_SLICE1_LOGS = 95 * KB


def tile_list_speech_noise_suppression_kernel(
    tc, tab_words, tab_scales, offs, offs2, w1, wgs, base, w4_words, w4_scales, out
):
    nc = tc.nc
    with ExitStack() as ctx:
        keep = ctx.enter_context(tc.tile_pool(name="keep", bufs=1))
        placed = ctx.enter_context(tc.tile_pool(name="placed", bufs=1))
        ring = ctx.enter_context(tc.tile_pool(name="ring", bufs=RING))
        stage = ctx.enter_context(tc.tile_pool(name="stage", bufs=STAGES))
        psum = ctx.enter_context(tc.psum_pool(name="psum", bufs=BANKS))

        def put(shape, dtype, name, at):
            return placed.tile(shape, dtype, name=name, offset=at, align_bytes=64)

        def load_w1(tile, a, half):
            nc.sync.dma_start(
                out=tile[:],
                in_=w1[a * P * PACK : (a + 1) * P * PACK, half * H // 2 : (half + 1) * H // 2].rearrange(
                    "(p j) c -> p j c", j=PACK
                ),
            )

        tab_s = keep.tile([P, T], U8, name="tab_s", align_bytes=64)
        nc.sync.dma_start(
            out=tab_s[0:QUAD, :].bitcast(I32), in_=tab_scales.rearrange("a q t -> q a t").bitcast(I32)
        )
        pick = keep.tile([P, S // PER_COL], U16, name="pick")
        nc.sync.dma_start(pick[:], offs)
        place = keep.tile([P, S // PER_COL], U16, name="place")
        nc.sync.dma_start(place[:], offs2)
        tab_w = [put([P, T], I32, "tab_w0", AT_TABLE[0]), put([P, T], I32, "tab_w1", AT_TABLE[1])]
        nc.sync.dma_start(out=tab_w[0][:], in_=tab_words[0].rearrange("p n i -> p (n i)").bitcast(I32))
        raw = {(a, 0): put([P, PACK, H // 2], F32, f"raw_low{a}", AT_RAW_LOW[a]) for a in range(PASSES)}
        for a in range(PASSES):
            load_w1(raw[a, 0], a, 0)
        nc.sync.dma_start(out=tab_w[1][:], in_=tab_words[1].rearrange("p n i -> p (n i)").bitcast(I32))

        nc.gpsimd.memset(tab_s[QUAD : 2 * QUAD, :].bitcast(I32), 0)
        nc.gpsimd.memset(tab_s[2 * QUAD : P, :].bitcast(I32), 0)
        v_s = [
            keep.tile([P, PASSES * BANK], U8, name="v_s0", align_bytes=64),
            put([P, PASSES * BANK], U8, "v_s1", AT_LATE_SCALES),
        ]
        nc.vector.memset(v_s[0][:].bitcast(I32), 0)
        warm = keep.tile([P, 2], F32, name="warm")
        nc.vector.memset(warm[:, 0:1], 1.0)
        nc.scalar.activation(out=warm[:, 1:2], in_=warm[:, 0:1], func=ACT.Ln)

        picked_s = keep.tile([P, S], U8, name="picked_s", tag="picked", align_bytes=64)
        nc.vector.tensor_copy(out=picked_s[:], in_=tab_s[:].indirect(pick[:]))

        def move_scales(b):
            for q in QUARTERS:
                nc.sync.dma_start(
                    out=v_s[b][QUAD * q : QUAD * q + 4, :].bitcast(I32),
                    in_=picked_s[8 * q : 8 * q + 8, b * BANK : (b + 1) * BANK].bitcast(I32),
                )

        move_scales(0)
        v_first = keep.tile([P, S], U32, name="v_first", align_bytes=64)
        nc.vector.tensor_copy(out=v_first[:], in_=tab_w[0][:].bitcast(U32).indirect(pick[:]))
        nc.vector.memset(v_s[1][:].bitcast(I32), 0)
        pages = [keep.tile([P, T2], F32, name=f"page{u}") for u in range(PAGES)]
        nc.vector.memset(pages[0][:], 0.0)
        for page in pages[1:]:
            nc.gpsimd.memset(page[:], 0.0)
        w4_s = keep.tile([P, N], U8, name="w4_s", align_bytes=64)
        nc.gpsimd.memset(w4_s[:].bitcast(I32), 0)

        w1_c = {
            (s, a): keep.tile([P, P], U32, name=f"w1_c{s}{a}", align_bytes=64)
            for s in range(PACK)
            for a in range(PASSES)
            if (s, a) != (1, 1)
        }
        w1_c[1, 1] = put([P, P], U32, "w1_c11", AT_LATE_CODES)
        w1_s = [keep.tile([P, PASSES * P], U8, name=f"w1_s{s}", align_bytes=64) for s in range(PACK)]
        grouped = {}

        def cast(a, half, t0, at, copy=nc.scalar.copy):
            grouped[a, half, t0] = put([P, 2 * MID * PACK], BF16, f"grouped{a}{half}{t0}", at)[:]
            copy(
                out=grouped[a, half, t0].rearrange("p (t u j) -> p u j t", t=2, j=PACK),
                in_=raw[a, half][:].rearrange("p j (u t) -> p u j t", t=PACK)[:, :, :, t0 : t0 + 2],
            )

        def cast_whole(a, half, at):
            whole = put([P, PACK * MID * PACK], BF16, f"whole{a}{half}", at)
            nc.scalar.copy(
                out=whole[:].rearrange("p (t u j) -> p u j t", t=PACK, j=PACK),
                in_=raw[a, half][:].rearrange("p j (u t) -> p u j t", t=PACK),
            )
            for t0 in (0, 2):
                grouped[a, half, t0] = whole[:, t0 * MID * PACK : (t0 + 2) * MID * PACK]

        def quantise(a, half, t0):
            src = grouped[a, half, t0]
            if t0 == 0:
                cols = slice(a * P, (a + 1) * P)
                nc.vector.quantize_mx(out=w1_c[half, a][:].bitcast(FP8X4), scales=w1_s[half][:, cols], in_=src)
            else:
                cols = slice(a * P + half * MID, a * P + (half + 1) * MID)
                for t in (2, 3):
                    nc.vector.quantize_mx(
                        out=w1_c[t, a][:, half * MID : (half + 1) * MID].bitcast(FP8X4),
                        scales=w1_s[t][:, cols],
                        in_=src[:, (t - 2) * MID * PACK : (t - 1) * MID * PACK],
                    )

        for a in range(PASSES):
            for t0 in (0, 2):
                cast(a, 0, t0, AT_ROUNDED_LOW[a] + t0 // 2 * KB)
                quantise(a, 0, t0)

        v_last = [keep.tile([P, BANK], U32, name=f"v_last{b}", align_bytes=64) for b in range(HALVES)]
        cols_per_half = BANK // PER_COL
        for b in range(HALVES):
            nc.vector.tensor_copy(
                out=v_last[b][:],
                in_=tab_w[1][:].bitcast(U32).indirect(pick[:, b * cols_per_half : (b + 1) * cols_per_half]),
            )

        wgs_rows = wgs.rearrange("(p t) j -> p t j", t=PACK)

        def load_wgs(tile, planes, j0, w):
            for q in QUARTERS:
                nc.sync.dma_start(
                    out=tile[QUAD * q : QUAD * (q + 1), :], in_=wgs_rows[:, planes[q // 2], j0 : j0 + w]
                )

        wg_low = put([P, S], F32, "wg_low", AT_WGS_LOW)
        for a in range(PASSES):
            raw[a, 1] = put([P, PACK, H // 2], F32, f"raw_high{a}", AT_RAW_HIGH[a])
            load_w1(raw[a, 1], a, 1)
            if a == 0:
                move_scales(1)
            load_wgs(wg_low[:, BANK * a : BANK * (a + 1)], (0, 1), BANK * a, BANK)
        wg_high = {t: put([P, S], F32, f"wg{t}", AT_WGS_HIGH[t]) for t in (2, 3)}
        for t in (2, 3):
            load_wgs(wg_high[t][:], (t, t), 0, S)
        w4_w = keep.tile([P, 2 * N], U8, name="w4_w", tag="picked", align_bytes=64)
        nc.sync.dma_start(out=w4_w[:].bitcast(I32), in_=w4_words[0].bitcast(I32))
        for q in range(P // QUAD):
            nc.sync.dma_start(
                out=w4_s[QUAD * q : QUAD * q + 4, :].bitcast(I32),
                in_=w4_scales[0, 4 * q : 4 * q + 4, :].bitcast(I32),
            )
        base_rows = base.rearrange("(p t) c -> p t c", t=PACK)
        spans = [(SOLO + WIDE * sum(GROUPS[:g]), WIDE * count) for g, count in enumerate(GROUPS)]
        base_low = {}

        def load_low(c0, w, at):
            base_low[c0] = put([P, 2, w], F32, f"base_low{c0}", at)
            nc.sync.dma_start(out=base_low[c0][:], in_=base_rows[:, 0:2, c0 : c0 + w])

        for c0, w in spans[:EARLY]:
            load_low(c0, w, AT_BASE_LOW + 2 * WORD * (c0 - SOLO))

        h = {s: keep.tile([P, S], F32, name=f"h{s}") for s in (0, 2, 3)}
        h_late = put([P, BANK], F32, "h_late", AT_LATE_LOGS)
        first_abs = put([P, S], F32, "first_abs", AT_FIRST_ABS)
        h[1] = put([P, S], F32, "h1", AT_SLICE1_LOGS)
        h_second = put([P, PIECE], F32, "h_second", AT_SECOND_LOGS)

        def logs(s, j0, w):
            return {(0, PIECE): h_second[:], (0, BANK): h_late[:]}.get((s, j0), h[s][:, j0 : j0 + w])

        last_abs = put([P, 2 * (spans[EARLY][0] - SOLO)], F32, "last_abs", AT_GAIN)
        parked_pairs = [
            put([P, 2 * (T2 - SOLO) + PACK * SOLO], F32, "parked0", AT_PARKED[0]),
            put([P, T2 - SOLO], F32, "parked1", AT_PARKED[1]),
        ]
        parked_solo = [put([P, SOLO], F32, f"parked_solo{t}", AT_PARKED_SOLO[t]) for t in range(2)]

        later = spans[EARLY][0]
        parked_first = put([P, 2 * (T2 - later)], F32, "parked_first", AT_GAIN + 2 * WORD * (later - SOLO))

        def parked(t, c0, w):
            if (t, c0) == (0, SOLO):
                return parked_first[:, 0:w]
            return parked_solo[t][:] if c0 < SOLO else parked_pairs[t][:, c0 - SOLO : c0 - SOLO + w]


        def make_h(s, j0, w):
            b, c0 = divmod(j0, BANK)
            y = psum.tile([P, BANK], F32, name="bank")
            moving = (v_first[:, j0 : j0 + w], v_last[b][:, c0 : c0 + w])
            order = (1, 0) if s == 0 and j0 > 0 else (0, 1)
            for a in order:
                nc.tensor.matmul_mx(
                    out=y[:, 0:w],
                    lhsT=w1_c[s, a][:].bitcast(FP8X4),
                    lhsT_scale=w1_s[s][:, a * P : (a + 1) * P],
                    rhs=moving[a].bitcast(FP8X4),
                    rhs_scale=v_s[b][:, a * BANK + c0 : a * BANK + c0 + w],
                    start=a == order[0],
                    stop=a == order[1],
                )
            if s == 0:
                magnitude = first_abs[:, 0:w]
            elif (s, j0 + w) == (PACK - 1, S):
                magnitude = last_abs[:, 0:w]
            else:
                magnitude = logs(s, j0, w)
            nc.scalar.activation(out=magnitude, in_=y[:, 0:w], func=ACT.Abs)
            nc.scalar.activation(out=logs(s, j0, w), in_=magnitude, func=ACT.Ln, bias=1.0)

        def scatter(s, j0, w):
            nc.vector.tensor_tensor(
                out=pages[s % PAGES][:].indirect(place[:, j0 // PER_COL : (j0 + w) // PER_COL]),
                in0=logs(s, j0, w),
                in1=(wg_low if s < 2 else wg_high[s])[:, j0 : j0 + w],
                op=MULT,
            )

        cast(0, 1, 0, AT_ROUNDED_HIGH[0], copy=nc.vector.tensor_copy)
        quantise(0, 1, 0)
        for j0 in (0, PIECE):
            make_h(0, j0, PIECE)
            scatter(0, j0, PIECE)
        cast_whole(1, 1, AT_ROUNDED_HIGH[1])
        quantise(1, 1, 0)
        make_h(0, BANK, BANK)
        scatter(0, BANK, BANK)
        second = spans[1][0]
        early = ((1, SOLO, T2 - SOLO), (0, SOLO, second - SOLO), (0, second, T2 - second), (1, 0, SOLO), (0, 0, SOLO))
        for t, c0, w in early:
            nc.sync.dma_start(out=parked(t, c0, w)[0:MID, :], in_=pages[0][MID * t : MID * (t + 1), c0 : c0 + w])
        cast(0, 1, 2, AT_FIRST_ABS)
        for a in range(PASSES):
            quantise(a, 1, 2)
        for s in (1, 2, 3):
            for j0 in (0, BANK):
                make_h(s, j0, BANK)

        def weigh(engine, s, j0, w):
            if s == 1:
                tile = put([P, (AT_BASE_LOW - AT_BASE) // WORD], F32, "weighted1", AT_BASE)[:, 0:w]
            else:
                tile = keep.tile([P, w], F32, name=f"weighted{s}_{j0}")[:]
            engine.tensor_tensor(
                out=tile, in0=h[s][:, j0 : j0 + w], in1=(wg_low if s < 2 else wg_high[s])[:, j0 : j0 + w], op=MULT
            )
            return tile

        def scatter_copy(s, j0, w, tile):
            nc.vector.tensor_copy(
                out=pages[s % PAGES][:].indirect(place[:, j0 // PER_COL : (j0 + w) // PER_COL]), in_=tile
            )

        scatter(1, 0, FUSED)
        scatter_copy(1, FUSED, S - FUSED, weigh(nc.vector, 1, FUSED, S - FUSED))
        for s in (2, 3):
            scatter_copy(s, 0, S, weigh(nc.gpsimd, s, 0, S))

        def make_gain(dst, src):
            nc.scalar.activation(out=dst, in_=src, func=ACT.Exp, scale=-1.0)

        for c0, w in spans + [(0, SOLO)]:
            if c0 < SOLO:
                for late, width in spans[EARLY:]:
                    load_low(late, width, AT_LATE_LOW + 2 * WORD * (late - SOLO))
            nc.sync.dma_start(out=parked(0, c0, w)[MID:P, :], in_=pages[1][0:MID, c0 : c0 + w])

        base_solo = put([P, PACK, SOLO], F32, "base_solo", AT_BASE)
        nc.sync.dma_start(out=base_solo[:], in_=base_rows[:, :, 0:SOLO])
        base_high = {}
        for c0, w in spans:
            base_high[c0] = put([P, 2, w], F32, f"base_high{c0}", AT_BASE + WORD * (PACK * SOLO + 2 * (c0 - SOLO)))
            nc.sync.dma_start(out=base_high[c0][:], in_=base_rows[:, 2:PACK, c0 : c0 + w])

        def plane1(dst, c0, w):
            make_gain(dst[0:MID, :], parked(1, c0, w)[0:MID, :])
            make_gain(dst[MID:P, :], pages[1][MID:P, c0 : c0 + w])

        low = [put([P, 2, w], F32, f"low{c0}", AT_GAIN + 2 * WORD * (c0 - SOLO)) for c0, w in spans]
        pairs = {}
        plane1(low[0][:, 1, :], *spans[0])
        for g, (c0, w) in enumerate(spans):
            if g == 0:
                plane1(low[1][:, 1, :], *spans[1])
            elif g > 1:
                plane1(low[g][:, 1, :], c0, w)
            make_gain(low[g][:, 0, :], parked(0, c0, w))
            both = keep.tile([P, 2, 2 * w], BF16, name=f"pairs{c0}")
            nc.gpsimd.tensor_tensor(
                out=both[:, 0, :].rearrange("p (c e t) -> p c t e", e=4, t=2),
                in0=low[g][:].rearrange("p t (c e) -> p c t e", e=4),
                in1=base_low[c0][:].rearrange("p t (c e) -> p c t e", e=4),
                op=MULT,
            )
            for k0 in range(0, w, WIDE):
                pairs[c0 + k0] = both[:, :, 2 * k0 : 2 * (k0 + WIDE)]
        solo = put([P, PACK, SOLO], F32, "solo", AT_SOLO)
        plane1(solo[:, 1, :], 0, SOLO)
        make_gain(solo[:, 0, :], parked(0, 0, SOLO))
        make_gain(solo[:, 2, :], pages[2][:, 0:SOLO])
        high = {}
        for c0, w in spans:
            high[c0] = put([P, 2, w], F32, f"high{c0}", AT_PARKED[0] + 2 * WORD * (c0 - SOLO))
            make_gain(high[c0][:, 0, :], pages[2][:, c0 : c0 + w])

        def upper(c0, w):
            if c0 < SOLO:
                return solo[:, :, c0 : c0 + w], base_solo[:, :, c0 : c0 + w]
            g0 = max(start for start in high if start <= c0)
            return high[g0][:, :, c0 - g0 : c0 - g0 + w], base_high[g0][:, :, c0 - g0 : c0 - g0 + w]

        def last_gain(i):
            c0, w = CHUNKS[i]
            make_gain(upper(c0, w)[0][:, 1 if c0 in pairs else PACK - 1, :], pages[0][:, c0 : c0 + w])

        for i in range(AHEAD):
            last_gain(i)

        out_rows = out.rearrange("(g p) c -> p g c", p=P)
        joined = {}
        for i, (c0, w) in enumerate(CHUNKS):
            z = ring.tile([P, PACK * w], BF16, name="z", align_bytes=64)
            gain, rows = upper(c0, w)
            planes = 2 if c0 in pairs else PACK
            product = pairs[c0][:, 1, :] if c0 in pairs else z[:]
            for f0, f1 in ((0, w // 2), (w // 2, w)) if i in (1, WOVEN_BY_SCALAR) else ((0, w),):
                nc.vector.tensor_tensor(
                    out=product[:, planes * f0 : planes * f1].rearrange("p (c e t) -> p c t e", e=2, t=planes),
                    in0=gain[:, :, f0:f1].rearrange("p t (c e) -> p c t e", e=2),
                    in1=rows[:, :, f0:f1].rearrange("p t (c e) -> p c t e", e=2),
                    op=MULT,
                )
            if c0 in pairs:
                weave = nc.scalar.copy if i == WOVEN_BY_SCALAR else nc.vector.tensor_copy
                words = U32 if i == WOVEN_BY_SCALAR else I32
                weave(
                    out=z[:].bitcast(words).rearrange("p (c u) -> p c u", u=2),
                    in_=pairs[c0].bitcast(words).rearrange("p u c -> p c u"),
                )
            z_c = ring.tile([P, w], U32, name="z_c", align_bytes=64)
            z_s = ring.tile([P, w], U8, name="z_s", align_bytes=64)
            nc.vector.quantize_mx(out=z_c[:].bitcast(FP8X4), scales=z_s[:], in_=z[:])
            turn = c0 // WIDE % 2 if c0 >= JOINED else 1
            for bank in (1 - turn, turn):
                g0 = bank * GROUPS_PER_BANK
                acc = psum.tile([P, BANK], F32, name="bank")
                for g in range(g0, g0 + GROUPS_PER_BANK):
                    nc.tensor.matmul_mx(
                        out=acc[:, (g - g0) * w : (g - g0 + 1) * w],
                        lhsT=w4_w[:, 2 * g * P : 2 * (g + 1) * P].bitcast(FP4X4),
                        lhsT_scale=w4_s[:, g * P : (g + 1) * P],
                        rhs=z_c[:].bitcast(FP8X4),
                        rhs_scale=z_s[:],
                        start=True,
                        stop=True,
                    )
                if bank in joined:
                    first_frame, width = c0 - w, 2 * w
                    res = joined[bank]
                    joined = {}
                elif c0 >= JOINED and c0 + w < T2 and bank == turn:
                    first_frame, width = c0, 2 * w
                    res = keep.tile([P, GROUPS_PER_BANK, width], F32, name=f"joined{c0}")
                    joined = {bank: res}
                else:
                    first_frame, width = c0, w
                    res = stage.tile([P, GROUPS_PER_BANK, w], F32, name="res")
                dst = res[:, :, c0 - first_frame : c0 - first_frame + w]
                src = acc[:, 0 : GROUPS_PER_BANK * w].rearrange("p (g c) -> p g c", g=GROUPS_PER_BANK)
                if i == len(CHUNKS) - 1 and bank != turn:
                    nc.vector.tensor_copy(out=dst, in_=src)
                else:
                    nc.scalar.copy(out=dst, in_=src)
                if c0 + w == first_frame + width:
                    nc.sync.dma_start(
                        out=out_rows[:, g0 : g0 + GROUPS_PER_BANK, first_frame : first_frame + width], in_=res[:]
                    )
            if i + AHEAD < len(CHUNKS):
                last_gain(i + AHEAD)
